import numpy as np
CORES = [24,26,29,31,48,50,53,55]
N = 8
T, EL, CAP, CAPP = 4096, 2, 1920, 512
E = N * EL
def entries(a): return a.T.reshape(-1)
def pack(v, P): return np.ascontiguousarray(np.asarray(v, np.int32).reshape(-1, P).T)
def lists(rng, how):
    g, q, h, R, K = CAP // CAPP, CAP % CAPP, E // 4, np.arange(N)[:, None], np.arange(E)
    C = np.zeros((N, E), np.int64); s = rng.integers(1, E, N); S = None
    few = rng.integers(1, CAPP // 4 + 1, (N, h)); t = rng.integers(CAPP // 8, 3 * CAPP // 8 + 1, (N, 3)); t[:, 2] = CAPP - t[:, 0] - t[:, 1]
    if how == "uniform":
        C[:, :h] = np.where(R <= g, CAPP, few); C[:, h:] = rng.integers(0, CAP // (2 * N) + 1, (N, E - h)); S = np.stack([rng.permutation(2 * h)[:3] + 1 for r in range(N)])
    if how == "bands":
        a = np.arange(E) % N; C = CAPP * ((R >= a) & (R <= a + g)); C[a[N:], np.arange(N, E)] = rng.integers(1, CAPP + 1, E - N); s[g:] = N - g + rng.integers(0, g, N - g) - np.arange(N - g)
    if how == "full":
        v = rng.integers(CAPP - q + 1, CAPP, h + 1); C[:, :h] = CAPP; C[:, h:2 * h + 1] = (CAP - v) // N; C[rng.integers(N), h:2 * h + 1] += (CAP - v) % N; s = h + (np.arange(N) + rng.integers(2)) % 2
    if how == "late":
        C[:N - 1, :h] = np.where(R <= g, CAPP, few)[:N - 1]; C[N - 1, h:3 * h] = rng.integers(1, CAPP + 1, 2 * h); s = rng.integers(h, 2 * h + 1, N)
    if how == "mesh":
        ev = np.arange(0, E, 2); P = np.stack([rng.permutation(2 * h) for r in range(N)]); S = 2 * P[:, :3] + 1; S[g] = 2 * rng.permutation(2 * h - 1)[:3] + 2
        C[:, ev] = CAPP; C[g, ev[h:]] = q; C[g, ev + 1] = rng.integers(0, (CAPP - q) // 2 + 1, 2 * h); C[g, 1] = 0
        z, y = g + 1 + int(rng.integers(0, g - 1)), 2 * int(rng.integers(1, 2 * h)) + 1; C[z, (y - 2 * P[z, 3] - 1) % E] = 0; C[z, y] = CAPP
    if how == "thin":
        C = rng.integers(0, CAP // N + 1, (N, E)); C[1] = 1; C[[0, N // 2, N - 1]] = 0
    if S is None: S, t = s[:, None], np.full((N, 1), CAPP)
    D = np.zeros((N, E, E), np.int64); Z = C.copy()
    for j in range(S.shape[1]):
        w = rng.integers(np.maximum(Z - t[:, j + 1:].sum(axis=1)[:, None], 0), np.minimum(Z, t[:, j:j + 1]) + 1); D[R, K, (K + S[:, j:j + 1]) % E] = w; Z -= w
    X = np.stack([rng.permutation(np.concatenate([np.repeat(np.arange(E * E), D[r].reshape(-1)), np.full(T - D[r].sum(), -1)])) for r in range(N)]); c = np.append(rng.permutation(E), -1)
    return {"e1": np.stack([pack(w, 16) for w in c[X // E]]), "e2": np.stack([pack(w, 16) for w in c[np.where(X < 0, -1, X % E)]])}
def blank(d):
    for r in range(0, N, 2):
        u, i = np.unique(entries(d["e1"][r])[::-1], return_index=True); d["x"][r][:, T - 1 - i[u >= 0]] = 0
def setup_inputs(rng):
    return dict({"x": rng.standard_normal((N, 128, T), dtype=np.float32)}, **lists(rng, "uniform"))
def setup_inputs_bands(rng):
    d = setup_inputs(rng); d.update(lists(rng, "bands"))
    for k in ("x",): d[k] = (d[k].astype(np.float32) * 1048576.0).astype(d[k].dtype)
    blank(d)
    return d
def setup_inputs_full(rng):
    d = setup_inputs(rng); d.update(lists(rng, "full"))
    for k in ("x",): d[k] = (d[k].astype(np.float32) * (1 / 1024.0)).astype(d[k].dtype)
    blank(d)
    return d
def setup_inputs_late(rng):
    d = setup_inputs(rng); d.update(lists(rng, "late"))
    blank(d)
    return d
def setup_inputs_mesh(rng):
    d = setup_inputs(rng); d.update(lists(rng, "mesh"))
    blank(d)
    return d
def setup_inputs_thin(rng):
    d = setup_inputs(rng); d.update(lists(rng, "thin"))
    blank(d)
    return d
def check_inputs(x):
    bad = []; a, b = x["e1"], x["e2"]
    if min(a.min(), b.min()) < -1 or max(a.max(), b.max()) >= E: bad.append("e1 or e2 out of range")
    if ((a < 0) != (b < 0)).any(): bad.append("-1 stands in one of e1 and e2 alone")
    if ((a == b) & (a >= 0)).any(): bad.append("a token's two choices are one expert")
    if max(int(np.bincount(v[v >= 0], minlength=E).max()) for w in (a, b) for v in w) > CAPP: bad.append("more than CAPP tokens of one rank have one expert as first choice, or as second choice")
    return bad
def places(e):
    o = np.argsort(e, kind="stable"); p = np.empty(len(e), np.int64); p[o] = np.arange(len(e)) - np.searchsorted(e[o], e[o]); return p
def reference(x, e1, e2):
    X = np.concatenate(list(x), axis=1); a, b = [np.concatenate([entries(v) for v in w]) for w in (e1, e2)]
    k = np.nonzero(a >= 0)[0]; p = places(a[k])
    c1 = np.minimum(np.bincount(a[k], minlength=E), CAP)
    f = k[p >= CAP]; u = c1[b[f]] + places(b[f])
    Y = np.zeros((128, E * CAP), x.dtype); m = p < CAP; Y[:, CAP * a[k[m]] + p[m]] = X[:, k[m]]
    n = u < CAP; Y[:, CAP * b[f[n]] + u[n]] = X[:, f[n]]
    return {"y": np.stack([Y[:, EL * CAP * r:EL * CAP * (r + 1)] for r in range(N)])}

@@ -1,0 +1,395 @@
+import numpy as np
+from concourse.bass import DstId, RemoteDMATransfer
+from concourse.mybir import dt, AluOpType, AxisListType, ActivationFunctionType
+
+N, TOK, E, CAP = 8, 4096, 16, 1920
+SLOTS = 2 * CAP
+NSIM = 64
+CHUNKS = [512, 1024, 1024, 1024, 512]
+STARTS = [sum(CHUNKS[:i]) for i in range(len(CHUNKS))]
+NCH = len(CHUNKS)
+BIG = 16384.0
+GCH = 960
+
+SCRATCH = {
+    "WIN": ("sbuf", [128, N * TOK + 8], "float32"),
+    "YB": ("sbuf", [128, SLOTS], "float32"),
+    "EI": ("sbuf", [128, N, 64], "int32"),
+    "PS": ("psum", [128, 4096], "float32"),
+    "PI": ("sbuf", [128, 1], "int32"),
+    "PJ": ("sbuf", [128, 4], "int32"),
+    "OFF": ("sbuf", [128, 256], "uint16"),
+    "SW": ("sbuf", [128, TOK + SLOTS], "bfloat16"),
+    "LST": ("sbuf", [128, SLOTS // 16], "uint16"),
+}
+for _n, _w in (("E1B", 256), ("E2B", 256), ("OH", E * 256), ("BB", E * 128), ("ZP", 248), ("TRI", 128), ("PW", 144),
+               ("VAL", 4096), ("DC", 256), ("JB", 512)):
+    SCRATCH[_n] = ("sbuf", [128, _w], "bfloat16")
+for _n, _w in (("BF", 512), ("PC", 4), ("PF", 1), ("M0", 128), ("M8", 128), ("M8S", 128), ("M16", 128), ("IA", 128),
+               ("IB", 128), ("HEQ", 128), ("TA", 128), ("TB", 128), ("OB", 128), ("TH", 128), ("MK", 16), ("CM", 128),
+               ("ON8", 8), ("RC", 2), ("PM", 4), ("WC", 12), ("C8", 8), ("U0", 128), ("UT", 128), ("UU", 512),
+               ("RM", 256), ("JJ", 256), ("SIN", 256), ("RI", 8), ("SF", 256), ("S1", 256), ("C1", 1), ("THR", 512),
+               ("ACC", 512), ("MM", 256), ("SIN2", 256), ("RI2", 8), ("S2", 256), ("G1", 512), ("A1", 512), ("B1", 256),
+               ("G2", 512), ("A2", 512), ("B2", 256)):
+    SCRATCH[_n] = ("sbuf", [128, _w], "float32")
+SEMAPHORES = (["le", "li", "lf", "xin", "sent", "sv", "st", "sa", "sg", "yd"]
+              + ["lx%d" % i for i in range(NCH)] + ["f%d" % i for i in range(NCH)] + ["h%d" % i for i in range(NCH)])
+
+
+def bits(mask):
+    return [b for b in range(mask.bit_length()) if mask >> b & 1]
+
+
+def unbits(bs):
+    return sum(1 << b for b in bs)
+
+
+def make_routes(cores, topo):
+    chips = sorted(set(topo.chip(c) for c in cores))
+    on = {ch: [c for c in range(NSIM) if topo.chip(c) == ch] for ch in set(topo.chip(c) for c in range(NSIM))}
+    far = {s: [ch for ch in chips if ch != topo.chip(cores[s])][0] for s in range(N)}
+    land, relay, fwd, peer, cross = {}, {}, {}, {}, {}
+    for d in (0, 1):
+        for ch in chips:
+            src = [s for s in range(N) if far[s] == ch and topo.die(cores[s]) == d]
+            hel = [c for c in on[ch] if c not in cores and topo.die(c) == d]
+            src.sort(key=lambda s: not topo.may_write(cores[s], hel[0]))
+            hel.sort(key=lambda c: topo.may_write(c, cores[src[0]]))
+            for s, hc in zip(src, hel):
+                land[s], relay[s], fwd[s] = hc, None, None
+                if not topo.may_write(cores[s], hc):
+                    mid = [m for m in on if topo.mates(m, ch) and topo.same_plane(m, topo.chip(cores[s]))][0]
+                    relay[s] = [c for c in on[mid] if topo.die(c) == d and topo.may_write(c, hc)][0]
+                    fwd[s] = [c for c in on[topo.chip(cores[s])] if c not in cores and topo.die(c) == d
+                              and topo.may_write(c, hc)][0]
+    for ch in chips:
+        die = [[s for s in range(N) if topo.chip(cores[s]) == ch and topo.die(cores[s]) == d] for d in (0, 1)]
+        for d in (0, 1):
+            for i in (0, 1):
+                peer[die[d][i]] = die[d][1 - i]
+                cross[die[d][i]] = die[1 - d][i]
+    return far, land, relay, fwd, peer, cross
+
+
+def rank_program(g, core, T, topo):
+    cores = list(T.cores)
+    far, land, relay, fwd, peer, cross = make_routes(cores, topo)
+    rank = T.rank_of(core)
+    sent = [0]
+
+    def ids(cs):
+        out = []
+        for c in cs:
+            rid, pid, _ = topo.addr(c)
+            out.append(DstId(rid=rid, pnc=pid))
+        return out
+
+    def write(buf, parts):
+        trs = []
+        for cs, eng, sem in parts:
+            trs.append(RemoteDMATransfer(dst_ids=ids(cs), dma_engine_mask=unbits(eng), remote_sem=T.sem[sem],
+                                         srcs=[buf], dsts=[buf for _ in cs]))
+            sent[0] += len(eng)
+        g.remote_dma_fused(trs, local_sem=T.sem.sent)
+
+    def xpart(s, i):
+        a = s * TOK + STARTS[i]
+        return T.WIN[:, a:a + CHUNKS[i]]
+
+    off_eng = bits(min(topo.mask(core, c) for c in range(NSIM) if c != core))
+    all_eng = bits(max(topo.mask(core, c) for c in range(NSIM) if c != core))
+    rest = [b for b in all_eng if b not in off_eng]
+
+    if rank is None:
+        for s in range(N):
+            if fwd[s] == core:
+                g.wait_ge(T.sem.lf, len(off_eng))
+                write(T.EI[:, s], [([c for c in cores if topo.chip(c) == far[s]], off_eng, "li")])
+        for s in range(N):
+            if relay[s] == core:
+                for i in range(NCH):
+                    g.wait_ge(T.sem["h%d" % i], len(off_eng))
+                    write(xpart(s, i), [([land[s]], off_eng, "h%d" % i)])
+            if land[s] == core:
+                here = [c for c in cores if topo.chip(c) == topo.chip(core)]
+                same = [c for c in here if topo.die(c) == topo.die(core)]
+                other = [c for c in here if topo.die(c) != topo.die(core)]
+                q = [all_eng[k::4] for k in range(4)]
+                for i in range(NCH):
+                    g.wait_ge(T.sem["h%d" % i], len(off_eng))
+                    write(xpart(s, i), [([other[0]], q[0], "xin"), ([same[0]], q[1], "xin"),
+                                        ([other[1]], q[2], "xin"), ([same[1]], q[3], "xin")])
+        if sent[0]:
+            g.wait_ge(T.sem.sent, sent[0])
+        return
+
+    g.sync.dma_start(T.EI[:, rank, 0:32], T.e1[:]).then_inc(T.sem.le, 16)
+    g.scalar.dma_start(T.EI[:, rank, 32:64], T.e2[:]).then_inc(T.sem.le, 16)
+    for i in range(NCH):
+        q = g.sync if i % 2 == 0 else g.scalar
+        q.dma_start(xpart(rank, i), T.x[:, STARTS[i]:STARTS[i] + CHUNKS[i]]).then_inc(T.sem["lx%d" % i], 16)
+
+    eng = {"v": g.vector, "t": g.tensor, "a": g.scalar, "g": g}
+    sem = {"v": T.sem.sv, "t": T.sem.st, "a": T.sem.sa, "g": T.sem.sg}
+    cnt = {"v": 0, "t": 0, "a": 0, "g": 0}
+    seen, wr, rd = {}, {}, {}
+
+    def op(q, fn, r, w):
+        need = {}
+
+        def dep(x):
+            if not (x[0] == q and q == "t"):
+                need[x[0]] = max(need.get(x[0], 0), x[1])
+        for t in r:
+            if t in wr:
+                dep(wr[t])
+        for t in w:
+            if t in wr:
+                dep(wr[t])
+            for x in rd.get(t, {}).items():
+                dep(x)
+        for k in sorted(need):
+            if seen.get((q, k), 0) < need[k]:
+                eng[q].wait_ge(sem[k], need[k])
+                seen[(q, k)] = need[k]
+        fn().then_inc(sem[q], 1)
+        cnt[q] += 1
+        for t in r:
+            rd.setdefault(t, {})[q] = cnt[q]
+        for t in w:
+            wr[t] = (q, cnt[q])
+            rd[t] = {}
+
+    def V(fn, r, w):
+        op("v", fn, r, w)
+
+    def ts(out, in0, s1, s2, op0, op1, r, w):
+        if op1 is None:
+            V(lambda: g.vector.tensor_scalar(out, in0, s1, s2, op0), r, w)
+        else:
+            V(lambda: g.vector.tensor_scalar(out, in0, s1, s2, op0, op1), r, w)
+
+    def tt(out, a, b, o, r, w):
+        V(lambda: g.vector.tensor_tensor(out, a, b, o), r, w)
+
+    def mm(out, lhsT, rhs, start, stop, r, w):
+        op("t", lambda: g.tensor.matmul(out, lhsT, rhs, start, stop), r, w)
+
+    def iota(out, pattern, cm, w):
+        op("g", lambda: g.iota(out, pattern, 0, cm, allow_small_or_imprecise_dtypes=True), [], [w])
+
+    def pb(b, x, y):
+        return T.PS[:, 512 * b + x:512 * b + y]
+
+    A = AluOpType
+    k0 = 2 * rank
+
+    iota(T.PI[:], [[1, 1]], 1, "PI")
+    iota(T.M0[:], [[1, 128]], 0, "M0")
+    iota(T.M8[:], [[0, 16], [1, 8]], 0, "M8")
+    iota(T.M8S[:], [[1, 16], [0, 8]], 0, "M8S")
+    me = topo.chip(core)
+    near = [c for c in cores if topo.chip(c) == me and c != core]
+    away = [c for c in cores if topo.chip(c) != me]
+    g.wait_ge(T.sem.le, 32)
+    if fwd[rank] is None:
+        write(T.EI[:, rank], [(away, off_eng, "li")])
+    else:
+        write(T.EI[:, rank], [([fwd[rank]], off_eng, "lf")])
+    write(T.EI[:, rank], [(near, off_eng, "li")])
+    iota(T.M16[:], [[0, 8], [1, 16]], 0, "M16")
+    iota(T.IA[:], [[1, 8], [0, 2], [32, 8]], 0, "IA")
+    iota(T.IB[:], [[0, 8], [1, 2], [0, 8]], 0, "IB")
+    out_to = relay[rank] if relay[rank] is not None else land[rank]
+    for i in range(NCH):
+        g.wait_ge(T.sem["lx%d" % i], 16)
+        write(xpart(rank, i), [([out_to], off_eng, "h%d" % i), ([cores[cross[rank]]], rest[0::2], "f%d" % i),
+                               ([cores[peer[rank]]], rest[1::2], "xin")])
+    got = [s for s in range(N) if cross[s] == rank][0]
+    for i in range(NCH):
+        g.wait_ge(T.sem["f%d" % i], len(rest[0::2]))
+        write(xpart(got, i), [([cores[peer[rank]]], off_eng, "xin")])
+
+    ts(T.PJ[:, 0:1], T.PI[:], 7, None, A.bitwise_and, None, ["PI"], ["PJ0"])
+    ts(T.PJ[:, 1:2], T.PI[:], 3, None, A.arith_shift_right, None, ["PI"], ["PJ1"])
+    ts(T.PJ[:, 2:3], T.PI[:], 15, None, A.bitwise_and, None, ["PI"], ["PJ2"])
+    ts(T.PJ[:, 3:4], T.PI[:], 4, None, A.arith_shift_right, None, ["PI"], ["PJ3"])
+    V(lambda: g.vector.tensor_copy(T.PF[:], T.PI[:]), ["PI"], ["PF"])
+    V(lambda: g.vector.tensor_copy(T.PC[:], T.PJ[:]), ["PJ0", "PJ1", "PJ2", "PJ3"], ["PC"])
+    P7, PS3, P15, PS4 = (T.PC[:, i:i + 1] for i in range(4))
+    ts(T.HEQ[:], T.M8[:], P7, None, A.is_equal, None, ["M8", "PC"], ["HEQ"])
+    ts(T.MK[:], T.M0[:, 0:16], PS3, None, A.is_equal, None, ["M0", "PC"], ["MK"])
+    for k in range(E):
+        op("a", lambda k=k: g.scalar.activation(T.BB[:, k * 128:(k + 1) * 128], T.HEQ[:], ActivationFunctionType.Copy,
+                                                scale=T.MK[:, k:k + 1]), ["HEQ", "MK"], ["BB%d" % k])
+    V(lambda: g.vector.memset(T.ZP[:], 0.0), [], ["ZP"])
+    V(lambda: g.vector.memset(T.CM[:], 0.0), [], ["CM"])
+    V(lambda: g.vector.memset(T.ON8[:], 1.0), [], ["ON8"])
+    V(lambda: g.vector.memset(T.RM[:], 1.0), [], ["RM"])
+    V(lambda: g.vector.tensor_copy(T.ZP[:, 120:128], T.HEQ[:, 0:8]), ["HEQ"], ["ZP"])
+    ts(T.TA[:], T.M0[:], T.PF[:], None, A.is_lt, None, ["M0", "PF"], ["TA"])
+    ts(T.TB[:], T.M0[:], T.PF[:], BIG, A.is_equal, A.mult, ["M0", "PF"], ["TB"])
+    ts(T.OB[:], T.M8S[:], PS3, None, A.is_equal, None, ["M8S", "PC"], ["OB"])
+    tt(T.TA[:], T.TA[:], T.HEQ[:], A.mult, ["TA", "HEQ"], ["TA"])
+    for i in range(2):
+        ts(T.CM[:, 8 * i:8 * i + 8], T.ON8[:], T.MK[:, k0 + i:k0 + i + 1], None, A.mult, None, ["ON8", "MK"], ["CM"])
+    tt(T.TRI[:], T.TB[:], T.TA[:], A.subtract, ["TA", "TB"], ["TRI"])
+    ts(T.TB[:], T.M0[:], T.PF[:], -1.0, A.is_le, A.mult, ["M0", "PF"], ["TB"])
+    for r in range(N):
+        V(lambda r=r: g.vector.memset(T.RM[:, 32 * r:32 * r + 1], 0.0), ["RM"] if r == 0 else [], ["RM%d" % r])
+    RMT = ["RM"] + ["RM%d" % r for r in range(N)]
+    tt(T.TH[:], T.TB[:], T.OB[:], A.mult, ["TB", "OB"], ["TH"])
+    base = float(TOK - BIG - 1)
+    ts(T.RC[:, 0:1], T.MK[:, k0 + 1:k0 + 2], float(CAP), base, A.mult, A.add, ["MK"], ["RC0"])
+    ts(T.RC[:, 1:2], T.MK[:, 1:2], float(CAP), base, A.mult, A.add, ["MK"], ["RC1"])
+    for n, k in enumerate((k0, k0 + 1, 0, 1)):
+        ts(T.BF[:, n * 128:(n + 1) * 128], T.HEQ[:], T.MK[:, k:k + 1], None, A.mult, None, ["HEQ", "MK"], ["BF%d" % n])
+    V(lambda: g.vector.memset(T.SW[:, TOK:], 0.0), [], ["SW"])
+    V(lambda: g.vector.memset(T.WIN[:, N * TOK:], 0.0), [], ["WZ"])
+    ts(T.PM[:], T.M0[:, 0:4], P15, None, A.is_equal, None, ["M0", "PC"], ["PM"])
+    ts(T.WC[:, 4:5], PS4, 2.0, None, A.mult, None, ["PC"], ["WC4"])
+    ts(T.C8[:], T.M0[:, 0:8], -1.0, 8.0, A.mult, A.add, ["M0"], ["C8"])
+    ts(T.WC[:, 0:1], T.PM[:, 0:1], -4096.0, None, A.mult, None, ["PM"], ["WC0"])
+    ts(T.UT[:], T.IB[:], T.PM[:, 2:3], T.PM[:, 3:4], A.mult, A.add, ["IB", "PM"], ["UT"])
+    ts(T.U0[:], T.IA[:], T.PM[:, 1:2], None, A.mult, None, ["IA", "PM"], ["U0"])
+    ts(T.WC[:, 1:2], T.PM[:, 1:2], 16.0, T.WC[:, 0:1], A.mult, A.add, ["PM", "WC0"], ["WC1"])
+    ts(T.C8[:], T.C8[:], T.PM[:, 0:1], None, A.mult, None, ["PM", "C8"], ["C8"])
+    tt(T.U0[:], T.U0[:], T.UT[:], A.add, ["U0", "UT"], ["U0"])
+    ts(T.WC[:, 2:3], T.PM[:, 2:3], 1.0, T.WC[:, 1:2], A.mult, A.add, ["PM", "WC1"], ["WC2"])
+    for b in range(4):
+        ts(T.WC[:, 5 + b:6 + b], T.PM[:, 1:2], 8.0 * b, None, A.mult, None, ["PM"], ["WB%d" % b])
+    ts(T.WC[:, 3:4], T.PM[:, 3:4], T.WC[:, 4:5], T.WC[:, 2:3], A.mult, A.add, ["PM", "WC2", "WC4"], ["WC3"])
+    for b in range(4):
+        ts(T.UU[:, 128 * b:128 * b + 128], T.U0[:], T.WC[:, 5 + b:6 + b], None, A.add, None, ["U0", "WB%d" % b],
+           ["UU%d" % b])
+    for r in range(N):
+        op("a", lambda r=r: g.scalar.activation(T.VAL[:, 512 * r:512 * r + 512], T.UU[:], ActivationFunctionType.Identity,
+                                                bias=T.C8[:, r:r + 1]),
+           ["C8", "UU0", "UU1", "UU2", "UU3"], ["VAL%d" % r])
+    ts(T.PW[:, 0:128], T.M16[:], 0.0, T.WC[:, 3:4], A.is_equal, A.mult, ["M16", "WC3"], ["PW0"])
+    ts(T.PW[:, 128:144], T.M16[:, 0:16], 0.0, T.WC[:, 3:4], A.is_equal, A.mult, ["M16", "WC3"], ["PW1"])
+    ts(T.JJ[:, 0:128], T.M0[:], 16.0, P15, A.mult, A.add, ["M0", "PC"], ["JJ0"])
+    ts(T.JJ[:, 128:256], T.JJ[:, 0:128], 2048.0, None, A.add, None, ["JJ0"], ["JJ1"])
+
+    g.vector.wait_ge(T.sem.le, 32)
+    g.vector.wait_ge(T.sem.li, 7 * len(off_eng))
+    V(lambda: g.vector.tensor_copy(T.E1B[:], T.EI[:, :, 0:32]), [], ["E1B"])
+    V(lambda: g.vector.tensor_copy(T.E2B[:], T.EI[:, :, 32:64]), [], ["E2B"])
+
+    def oh(k):
+        return T.OH[:, k * 256:(k + 1) * 256]
+
+    def tri(b):
+        mm(pb(b, 0, 512), T.TRI[:], T.OH[:, b * 512:(b + 1) * 512], True, False,
+           ["TRI", "OH%d" % (2 * b), "OH%d" % (2 * b + 1)], ["pb%d" % b])
+
+    def add_columns(b):
+        for n in range(2):
+            k = 2 * b + n
+            mm(pb(b, n * 256, n * 256 + 256), T.BB[:, k * 128:(k + 1) * 128], T.DC[:], False, n == 1,
+               ["BB%d" % k, "DC"], ["pb%d" % b])
+
+    def offsets(out, sin, ri, tag, r):
+        mm(out, T.TH[:], sin[:, 31:256:32], True, False, ["TH"] + r, [tag])
+        mm(out, T.OB[:], ri[:], False, True, ["OB"] + r, [tag])
+
+    for k in range(E):
+        ts(oh(k), T.E1B[:], float(k), None, A.is_equal, None, ["E1B"], ["OH%d" % k])
+        mm(pb(7, 0, 256), T.ZP[:, 120 - 8 * k:248 - 8 * k], oh(k), k == 0, k == E - 1, ["ZP", "OH%d" % k], ["pb7"])
+    for b in range(3):
+        tri(b)
+    for i in range(2):
+        ts(T.THR[:, 256 * i:256 * i + 256], T.E2B[:], float(k0 + i), 1.0e5, A.not_equal, A.mult, ["E2B"], ["THR%d" % i])
+    for i in range(2):
+        ts(T.THR[:, 256 * i:256 * i + 256], T.THR[:, 256 * i:256 * i + 256], BIG + 1, None, A.add, None, ["THR%d" % i],
+           ["THR%d" % i])
+    V(lambda: g.vector.tensor_tensor_scan(T.SIN[:], T.RM[:], pb(7, 0, 256), 0.0, A.mult, A.add), ["pb7"] + RMT, ["SIN"])
+    V(lambda: g.vector.tensor_tensor_scan(T.RI[:], T.ON8[:], T.SIN[:, 31:256:32], 0.0, A.mult, A.add), ["SIN", "ON8"],
+      ["RI"])
+    offsets(pb(7, 256, 264), T.SIN, T.RI, "pb7", ["SIN", "RI"])
+    mm(pb(7, 264, 265), T.CM[:], T.RI[:, 7:8], True, True, ["CM", "RI"], ["pb7"])
+    for b in range(3, 7):
+        tri(b)
+    for r in range(N):
+        ts(T.SF[:, 32 * r:32 * r + 32], T.SIN[:, 32 * r:32 * r + 32], pb(7, 256 + r, 257 + r), None, A.add, None,
+           ["SIN", "pb7"], ["SF%d" % r])
+    SFT = ["SF%d" % r for r in range(N)]
+    ts(T.DC[:], T.SF[:], float(CAP + 16), float(CAP), A.min, A.subtract, SFT, ["DC"])
+    ts(T.C1[:], pb(7, 264, 265), float(CAP), T.RC[:, 1:2], A.min, A.add, ["pb7", "RC1"], ["C1"])
+    ts(T.S1[:], T.SF[:], T.RC[:, 0:1], None, A.add, None, SFT + ["RC0"], ["S1"])
+    for b in range(8):
+        if b == 7:
+            tri(7)
+        add_columns(b)
+        if b == 0:
+            V(lambda: g.vector.tensor_copy(T.ACC[:], pb(0, 0, 512)), ["pb0"], ["ACC"])
+        else:
+            tt(T.ACC[:], T.ACC[:], pb(b, 0, 512), A.max, ["ACC", "pb%d" % b], ["ACC"])
+    mm(pb(0, 0, 512), T.TRI[:], T.OH[:, k0 * 256:k0 * 256 + 512], True, False,
+       ["TRI", "OH%d" % k0, "OH%d" % (k0 + 1)], ["pb0"])
+    for i in range(2):
+        mm(pb(0, 256 * i, 256 * i + 256), T.BF[:, i * 128:(i + 1) * 128], T.S1[:], False, i == 1, ["BF%d" % i, "S1"],
+           ["pb0"])
+
+    tt(T.MM[:], T.ACC[:, 0:256], T.ACC[:, 256:512], A.max, ["ACC"], ["MM"])
+    for i in range(2):
+        tt(T.JB[:, 256 * i:256 * i + 256], T.MM[:], T.THR[:, 256 * i:256 * i + 256], A.is_ge, ["MM", "THR%d" % i],
+           ["JB%d" % i])
+        mm(pb(1, 0, 256), T.ZP[:, 120 - 8 * i:248 - 8 * i], T.JB[:, 256 * i:256 * i + 256], i == 0, i == 1,
+           ["ZP", "JB%d" % i], ["pb1"])
+    mm(pb(3, 0, 512), T.TRI[:], T.JB[:], True, False, ["TRI", "JB0", "JB1"], ["pb3"])
+    V(lambda: g.vector.tensor_tensor_scan(T.SIN2[:], T.RM[:], pb(1, 0, 256), 0.0, A.mult, A.add), ["pb1"] + RMT, ["SIN2"])
+    V(lambda: g.vector.tensor_tensor_scan(T.RI2[:], T.ON8[:], T.SIN2[:, 31:256:32], 0.0, A.mult, A.add), ["SIN2", "ON8"],
+      ["RI2"])
+    offsets(pb(2, 0, 8), T.SIN2, T.RI2, "pb2", ["SIN2", "RI2"])
+    for r in range(N):
+        ts(T.S2[:, 32 * r:32 * r + 32], T.SIN2[:, 32 * r:32 * r + 32], pb(2, r, r + 1), T.C1[:], A.add, A.add,
+           ["SIN2", "pb2", "C1"], ["S2%d" % r])
+    S2T = ["S2%d" % r for r in range(N)]
+    for i in range(2):
+        mm(pb(3, 256 * i, 256 * i + 256), T.BF[:, (2 + i) * 128:(3 + i) * 128], T.S2[:], False, i == 1,
+           ["BF%d" % (2 + i)] + S2T, ["pb3"])
+
+    def taken(bank, G, AA, n):
+        for i in range(2):
+            ts(G[:, 256 * i:256 * i + 256], pb(bank, 256 * i, 256 * i + 256), float(TOK + CAP * (i + 1)), None, A.is_lt,
+               None, ["pb%d" % bank], ["G%d%d" % (n, i)])
+        tt(AA[:], G[:], pb(bank, 0, 512), A.mult, ["G%d0" % n, "G%d1" % n, "pb%d" % bank], ["A%d" % n])
+
+    taken(0, T.G1, T.A1, 1)
+    tt(T.B1[:], T.A1[:, 0:256], T.A1[:, 256:512], A.max, ["A1"], ["B1"])
+    tt(T.B1[:], T.B1[:], T.JJ[:], A.max, ["B1", "JJ0", "JJ1"], ["B1"])
+    taken(3, T.G2, T.A2, 2)
+    tt(T.B2[:], T.A2[:, 0:256], T.A2[:, 256:512], A.max, ["A2"], ["B2"])
+    tt(T.B2[:], T.B2[:], T.B1[:], A.max, ["B2", "B1"], ["B2"])
+    V(lambda: g.vector.tensor_copy(T.OFF[:], T.B2[:]), ["B2"], ["OFF"])
+
+    V(lambda: g.vector.tensor_copy(T.SW[:, 0:TOK + SLOTS].indirect(T.OFF[:, 0:256]), T.VAL[:]),
+      ["OFF"] + ["VAL%d" % r for r in range(N)], ["SW"])
+    for q in range(16):
+        mm(pb(4, 0, SLOTS // 16), T.PW[:, 16 - q:144 - q], T.SW[:, TOK + q:TOK + SLOTS:16], q == 0, q == 15,
+           ["PW0", "PW1", "SW"], ["pb4"])
+    ts(T.LST[:], pb(4, 0, SLOTS // 16), float(N * TOK), None, A.add, None, ["pb4"], ["LST"])
+
+    n_x = NCH * (len(rest[1::2]) + len(off_eng) + 4 * (len(all_eng) // 4))
+    for q in ("v", "a"):
+        for i in range(NCH):
+            eng[q].wait_ge(T.sem["lx%d" % i], 16)
+            eng[q].wait_ge(T.sem["f%d" % i], len(rest[0::2]))
+        eng[q].wait_ge(T.sem.xin, n_x)
+    nst = 0
+    for n in range(SLOTS // GCH):
+        a, b = n * GCH, (n + 1) * GCH
+        src, out, tags = T.WIN[:, 0:N * TOK + 8].indirect(T.LST[:, a // 16:b // 16]), T.YB[:, a:b], ["LST", "WZ"]
+        if n % 2 == 0:
+            V(lambda: g.vector.tensor_copy(out, src), tags, ["Y%d" % n])
+        else:
+            op("a", lambda: g.scalar.activation(out, src, ActivationFunctionType.Copy), tags, ["Y%d" % n])
+        q, c = wr["Y%d" % n]
+        g.sync.wait_ge(sem[q], c)
+        g.sync.dma_start(T.y[:, a:b], out).then_inc(T.sem.yd, 16)
+        nst += 16
+    g.sync.wait_ge(T.sem.yd, nst)
+    for q in ("v", "t", "a", "g"):
+        g.wait_ge(sem[q], cnt[q])
+    g.wait_ge(T.sem.sent, sent[0])

@@ -2,13 +2,16 @@ import numpy as np
 from concourse.bass import DstId, RemoteDMATransfer
 from concourse.mybir import dt, AluOpType, AxisListType, ActivationFunctionType
 
-N, TOK, E, CAP = 8, 4096, 16, 1920
+N, TOK, E, CAP, CAPP = 8, 4096, 16, 1920, 512
 SLOTS = 2 * CAP
 NSIM = 64
-CHUNKS = [512, 1024, 1024, 1024, 512]
+CHUNKS = [384, 768, 768, 768, 768, 640]
 STARTS = [sum(CHUNKS[:i]) for i in range(len(CHUNKS))]
 NCH = len(CHUNKS)
-BIG = 16384.0
+VIA = [0]
+CUT = [1, 2, 3, 4, 5]
+BIG = 32768.0
+ROOM = CAP + N * CAPP
 GCH = 960
 
 SCRATCH = {
@@ -19,7 +22,7 @@ SCRATCH = {
     "PI": ("sbuf", [128, 1], "int32"),
     "PJ": ("sbuf", [128, 4], "int32"),
     "OFF": ("sbuf", [128, 256], "uint16"),
-    "SW": ("sbuf", [128, TOK + SLOTS], "bfloat16"),
+    "SW": ("sbuf", [128, TOK + 2 * ROOM], "bfloat16"),
     "LST": ("sbuf", [128, SLOTS // 16], "uint16"),
 }
 for _n, _w in (("E1B", 256), ("E2B", 256), ("OH", E * 256), ("BB", E * 128), ("ZP", 248), ("TRI", 128), ("PW", 144),
@@ -29,11 +32,11 @@ for _n, _w in (("BF", 512), ("PC", 4), ("PF", 1), ("M0", 128), ("M8", 128), ("M8
                ("IB", 128), ("HEQ", 128), ("TA", 128), ("TB", 128), ("OB", 128), ("TH", 128), ("MK", 16), ("CM", 128),
                ("ON8", 8), ("RC", 2), ("PM", 4), ("WC", 12), ("C8", 8), ("U0", 128), ("UT", 128), ("UU", 512),
                ("RM", 256), ("JJ", 256), ("SIN", 256), ("RI", 8), ("SF", 256), ("S1", 256), ("C1", 1), ("THR", 512),
-               ("ACC", 512), ("MM", 256), ("SIN2", 256), ("RI2", 8), ("S2", 256), ("G1", 512), ("A1", 512), ("B1", 256),
-               ("G2", 512), ("A2", 512), ("B2", 256)):
+               ("ACC", 512), ("SIN2", 256), ("RI2", 8), ("OF2", 8), ("S2", 256), ("G1", 512), ("B1", 256), ("B2", 256)):
     SCRATCH[_n] = ("sbuf", [128, _w], "float32")
 SEMAPHORES = (["le", "li", "lf", "xin", "sent", "sv", "st", "sa", "sg", "yd"]
-              + ["lx%d" % i for i in range(NCH)] + ["f%d" % i for i in range(NCH)] + ["h%d" % i for i in range(NCH)])
+              + ["lx%d" % i for i in range(NCH)] + ["f%d" % i for i in range(NCH)] + ["h%d" % i for i in range(NCH)]
+              + ["o%d" % i for i in range(NCH)] + ["k%d" % i for i in range(NCH)] + ["go%d" % i for i in range(NCH - 1)])
 
 
 def bits(mask):
@@ -48,7 +51,7 @@ def make_routes(cores, topo):
     chips = sorted(set(topo.chip(c) for c in cores))
     on = {ch: [c for c in range(NSIM) if topo.chip(c) == ch] for ch in set(topo.chip(c) for c in range(NSIM))}
     far = {s: [ch for ch in chips if ch != topo.chip(cores[s])][0] for s in range(N)}
-    land, relay, fwd, peer, cross = {}, {}, {}, {}, {}
+    land, relay, peer, cross, via = {}, {}, {}, {}, {}
     for d in (0, 1):
         for ch in chips:
             src = [s for s in range(N) if far[s] == ch and topo.die(cores[s]) == d]
@@ -56,24 +59,25 @@ def make_routes(cores, topo):
             src.sort(key=lambda s: not topo.may_write(cores[s], hel[0]))
             hel.sort(key=lambda c: topo.may_write(c, cores[src[0]]))
             for s, hc in zip(src, hel):
-                land[s], relay[s], fwd[s] = hc, None, None
+                land[s], relay[s] = hc, None
                 if not topo.may_write(cores[s], hc):
                     mid = [m for m in on if topo.mates(m, ch) and topo.same_plane(m, topo.chip(cores[s]))][0]
                     relay[s] = [c for c in on[mid] if topo.die(c) == d and topo.may_write(c, hc)][0]
-                    fwd[s] = [c for c in on[topo.chip(cores[s])] if c not in cores and topo.die(c) == d
-                              and topo.may_write(c, hc)][0]
+            own = [s for s in range(N) if topo.chip(cores[s]) == ch and topo.die(cores[s]) == d]
+            for s, hc in zip(own, hel):
+                via[s] = hc
     for ch in chips:
         die = [[s for s in range(N) if topo.chip(cores[s]) == ch and topo.die(cores[s]) == d] for d in (0, 1)]
         for d in (0, 1):
             for i in (0, 1):
                 peer[die[d][i]] = die[d][1 - i]
                 cross[die[d][i]] = die[1 - d][i]
-    return far, land, relay, fwd, peer, cross
+    return land, relay, peer, cross, via
 
 
 def rank_program(g, core, T, topo):
     cores = list(T.cores)
-    far, land, relay, fwd, peer, cross = make_routes(cores, topo)
+    land, relay, peer, cross, via = make_routes(cores, topo)
     rank = T.rank_of(core)
     sent = [0]
 
@@ -96,29 +100,46 @@ def rank_program(g, core, T, topo):
         a = s * TOK + STARTS[i]
         return T.WIN[:, a:a + CHUNKS[i]]
 
+    def pieces(s, i):
+        k = 2 if relay[s] is not None and i in CUT else 1
+        a, w = s * TOK + STARTS[i], CHUNKS[i] // k
+        return [(T.WIN[:, a + j * w:a + (j + 1) * w], ("h%d", "k%d")[j] % i) for j in range(k)]
+
     off_eng = bits(min(topo.mask(core, c) for c in range(NSIM) if c != core))
     all_eng = bits(max(topo.mask(core, c) for c in range(NSIM) if c != core))
     rest = [b for b in all_eng if b not in off_eng]
+    q4 = [all_eng[k::4] for k in range(4)]
+    quarter = len(q4[0])
 
     if rank is None:
+        here = [c for c in cores if topo.chip(c) == topo.chip(core)]
+        same = [c for c in here if topo.die(c) == topo.die(core)]
+        other = [c for c in here if topo.die(c) != topo.die(core)]
         for s in range(N):
-            if fwd[s] == core:
+            if relay[s] == core:
                 g.wait_ge(T.sem.lf, len(off_eng))
-                write(T.EI[:, s], [([c for c in cores if topo.chip(c) == far[s]], off_eng, "li")])
+                write(T.EI[:, s], [([land[s]], off_eng, "lf")])
+            if land[s] == core:
+                g.wait_ge(T.sem.lf, len(off_eng))
+                write(T.EI[:, s], [([other[0]], q4[0], "li"), ([same[0]], q4[1], "li"),
+                                   ([other[1]], q4[2], "li"), ([same[1]], q4[3], "li")])
+        for s in range(N):
+            if via[s] == core:
+                for i in VIA:
+                    g.wait_ge(T.sem["o%d" % i], len(rest))
+                    write(xpart(s, i), [([other[0]], q4[0], "xin"), ([cores[peer[s]]], q4[1], "xin"),
+                                        ([other[1]], q4[2], "xin")])
         for s in range(N):
             if relay[s] == core:
                 for i in range(NCH):
-                    g.wait_ge(T.sem["h%d" % i], len(off_eng))
-                    write(xpart(s, i), [([land[s]], off_eng, "h%d" % i)])
+                    for p, first in pieces(s, i):
+                        g.wait_ge(T.sem[first], len(off_eng))
+                        write(p, [([land[s]], off_eng, "h%d" % i)])
             if land[s] == core:
-                here = [c for c in cores if topo.chip(c) == topo.chip(core)]
-                same = [c for c in here if topo.die(c) == topo.die(core)]
-                other = [c for c in here if topo.die(c) != topo.die(core)]
-                q = [all_eng[k::4] for k in range(4)]
                 for i in range(NCH):
-                    g.wait_ge(T.sem["h%d" % i], len(off_eng))
-                    write(xpart(s, i), [([other[0]], q[0], "xin"), ([same[0]], q[1], "xin"),
-                                        ([other[1]], q[2], "xin"), ([same[1]], q[3], "xin")])
+                    g.wait_ge(T.sem["h%d" % i], len(pieces(s, i)) * len(off_eng))
+                    write(xpart(s, i), [([other[0]], q4[0], "xin"), ([same[0]], q4[1], "xin"),
+                                        ([other[1]], q4[2], "xin"), ([same[1]], q4[3], "xin")])
         if sent[0]:
             g.wait_ge(T.sem.sent, sent[0])
         return
@@ -126,8 +147,9 @@ def rank_program(g, core, T, topo):
     g.sync.dma_start(T.EI[:, rank, 0:32], T.e1[:]).then_inc(T.sem.le, 16)
     g.scalar.dma_start(T.EI[:, rank, 32:64], T.e2[:]).then_inc(T.sem.le, 16)
     for i in range(NCH):
-        q = g.sync if i % 2 == 0 else g.scalar
-        q.dma_start(xpart(rank, i), T.x[:, STARTS[i]:STARTS[i] + CHUNKS[i]]).then_inc(T.sem["lx%d" % i], 16)
+        if i:
+            g.sync.wait_ge(T.sem["go%d" % (i - 1)], 1)
+        g.sync.dma_start(xpart(rank, i), T.x[:, STARTS[i]:STARTS[i] + CHUNKS[i]]).then_inc(T.sem["lx%d" % i], 16)
 
     eng = {"v": g.vector, "t": g.tensor, "a": g.scalar, "g": g}
     sem = {"v": T.sem.sv, "t": T.sem.st, "a": T.sem.sa, "g": T.sem.sg}
@@ -172,56 +194,69 @@ def rank_program(g, core, T, topo):
     def tt(out, a, b, o, r, w):
         V(lambda: g.vector.tensor_tensor(out, a, b, o), r, w)
 
+    def act(out, in_, scale, bias, r, w):
+        if bias is None:
+            op("a", lambda: g.scalar.activation(out, in_, ActivationFunctionType.Copy, scale=scale), r, w)
+        else:
+            op("a", lambda: g.scalar.activation(out, in_, ActivationFunctionType.Identity, bias=bias, scale=scale), r, w)
+
     def mm(out, lhsT, rhs, start, stop, r, w):
         op("t", lambda: g.tensor.matmul(out, lhsT, rhs, start, stop), r, w)
 
     def iota(out, pattern, cm, w):
         op("g", lambda: g.iota(out, pattern, 0, cm, allow_small_or_imprecise_dtypes=True), [], [w])
 
-    def pb(b, x, y):
-        return T.PS[:, 512 * b + x:512 * b + y]
+    def pb(b, x, y, step=1):
+        return T.PS[:, 512 * b + x:512 * b + y:step]
 
     A = AluOpType
     k0 = 2 * rank
 
     iota(T.PI[:], [[1, 1]], 1, "PI")
-    iota(T.M0[:], [[1, 128]], 0, "M0")
     iota(T.M8[:], [[0, 16], [1, 8]], 0, "M8")
+    iota(T.M0[:], [[1, 128]], 0, "M0")
     iota(T.M8S[:], [[1, 16], [0, 8]], 0, "M8S")
-    me = topo.chip(core)
-    near = [c for c in cores if topo.chip(c) == me and c != core]
-    away = [c for c in cores if topo.chip(c) != me]
-    g.wait_ge(T.sem.le, 32)
-    if fwd[rank] is None:
-        write(T.EI[:, rank], [(away, off_eng, "li")])
-    else:
-        write(T.EI[:, rank], [([fwd[rank]], off_eng, "lf")])
-    write(T.EI[:, rank], [(near, off_eng, "li")])
-    iota(T.M16[:], [[0, 8], [1, 16]], 0, "M16")
-    iota(T.IA[:], [[1, 8], [0, 2], [32, 8]], 0, "IA")
-    iota(T.IB[:], [[0, 8], [1, 2], [0, 8]], 0, "IB")
+    near = [c for c in cores if topo.chip(c) == topo.chip(core) and c != core]
     out_to = relay[rank] if relay[rank] is not None else land[rank]
+    g.wait_ge(T.sem.le, 32)
+    write(T.EI[:, rank], [([out_to], off_eng, "lf")])
+    write(T.EI[:, rank], [(near, rest, "li")])
+    g.sem_inc(T.sem.go0, 1)
     for i in range(NCH):
         g.wait_ge(T.sem["lx%d" % i], 16)
-        write(xpart(rank, i), [([out_to], off_eng, "h%d" % i), ([cores[cross[rank]]], rest[0::2], "f%d" % i),
-                               ([cores[peer[rank]]], rest[1::2], "xin")])
+        if i in VIA:
+            local = [([via[rank]], rest, "o%d" % i)]
+        else:
+            local = [([cores[cross[rank]]], rest[0::2], "f%d" % i), ([cores[peer[rank]]], rest[1::2], "xin")]
+        ps = pieces(rank, i)
+        if len(ps) == 1:
+            write(xpart(rank, i), [([out_to], off_eng, ps[0][1])] + local)
+        else:
+            for p, first in ps:
+                write(p, [([out_to], off_eng, first)])
+            write(xpart(rank, i), local)
+        if i + 1 < NCH - 1:
+            g.sem_inc(T.sem["go%d" % (i + 1)], 1)
+        if i == 0:
+            iota(T.M16[:], [[0, 8], [1, 16]], 0, "M16")
+        if i == 1:
+            iota(T.IA[:], [[1, 8], [0, 2], [32, 8]], 0, "IA")
+            iota(T.IB[:], [[0, 8], [1, 2], [0, 8]], 0, "IB")
     got = [s for s in range(N) if cross[s] == rank][0]
     for i in range(NCH):
-        g.wait_ge(T.sem["f%d" % i], len(rest[0::2]))
-        write(xpart(got, i), [([cores[peer[rank]]], off_eng, "xin")])
+        if i not in VIA:
+            g.wait_ge(T.sem["f%d" % i], len(rest[0::2]))
+            write(xpart(got, i), [([cores[peer[rank]]], off_eng, "xin")])
 
     ts(T.PJ[:, 0:1], T.PI[:], 7, None, A.bitwise_and, None, ["PI"], ["PJ0"])
     ts(T.PJ[:, 1:2], T.PI[:], 3, None, A.arith_shift_right, None, ["PI"], ["PJ1"])
     ts(T.PJ[:, 2:3], T.PI[:], 15, None, A.bitwise_and, None, ["PI"], ["PJ2"])
     ts(T.PJ[:, 3:4], T.PI[:], 4, None, A.arith_shift_right, None, ["PI"], ["PJ3"])
-    V(lambda: g.vector.tensor_copy(T.PF[:], T.PI[:]), ["PI"], ["PF"])
     V(lambda: g.vector.tensor_copy(T.PC[:], T.PJ[:]), ["PJ0", "PJ1", "PJ2", "PJ3"], ["PC"])
     P7, PS3, P15, PS4 = (T.PC[:, i:i + 1] for i in range(4))
+    V(lambda: g.vector.tensor_copy(T.PF[:], T.PI[:]), ["PI"], ["PF"])
     ts(T.HEQ[:], T.M8[:], P7, None, A.is_equal, None, ["M8", "PC"], ["HEQ"])
     ts(T.MK[:], T.M0[:, 0:16], PS3, None, A.is_equal, None, ["M0", "PC"], ["MK"])
-    for k in range(E):
-        op("a", lambda k=k: g.scalar.activation(T.BB[:, k * 128:(k + 1) * 128], T.HEQ[:], ActivationFunctionType.Copy,
-                                                scale=T.MK[:, k:k + 1]), ["HEQ", "MK"], ["BB%d" % k])
     V(lambda: g.vector.memset(T.ZP[:], 0.0), [], ["ZP"])
     V(lambda: g.vector.memset(T.CM[:], 0.0), [], ["CM"])
     V(lambda: g.vector.memset(T.ON8[:], 1.0), [], ["ON8"])
@@ -231,50 +266,40 @@ def rank_program(g, core, T, topo):
     ts(T.TB[:], T.M0[:], T.PF[:], BIG, A.is_equal, A.mult, ["M0", "PF"], ["TB"])
     ts(T.OB[:], T.M8S[:], PS3, None, A.is_equal, None, ["M8S", "PC"], ["OB"])
     tt(T.TA[:], T.TA[:], T.HEQ[:], A.mult, ["TA", "HEQ"], ["TA"])
-    for i in range(2):
-        ts(T.CM[:, 8 * i:8 * i + 8], T.ON8[:], T.MK[:, k0 + i:k0 + i + 1], None, A.mult, None, ["ON8", "MK"], ["CM"])
+    V(lambda: g.vector.memset(T.RM[:, 0:256:32], 0.0), [], ["RM"])
     tt(T.TRI[:], T.TB[:], T.TA[:], A.subtract, ["TA", "TB"], ["TRI"])
     ts(T.TB[:], T.M0[:], T.PF[:], -1.0, A.is_le, A.mult, ["M0", "PF"], ["TB"])
-    for r in range(N):
-        V(lambda r=r: g.vector.memset(T.RM[:, 32 * r:32 * r + 1], 0.0), ["RM"] if r == 0 else [], ["RM%d" % r])
-    RMT = ["RM"] + ["RM%d" % r for r in range(N)]
-    tt(T.TH[:], T.TB[:], T.OB[:], A.mult, ["TB", "OB"], ["TH"])
-    base = float(TOK - BIG - 1)
-    ts(T.RC[:, 0:1], T.MK[:, k0 + 1:k0 + 2], float(CAP), base, A.mult, A.add, ["MK"], ["RC0"])
-    ts(T.RC[:, 1:2], T.MK[:, 1:2], float(CAP), base, A.mult, A.add, ["MK"], ["RC1"])
-    for n, k in enumerate((k0, k0 + 1, 0, 1)):
-        ts(T.BF[:, n * 128:(n + 1) * 128], T.HEQ[:], T.MK[:, k:k + 1], None, A.mult, None, ["HEQ", "MK"], ["BF%d" % n])
-    V(lambda: g.vector.memset(T.SW[:, TOK:], 0.0), [], ["SW"])
     V(lambda: g.vector.memset(T.WIN[:, N * TOK:], 0.0), [], ["WZ"])
+    tt(T.TH[:], T.TB[:], T.OB[:], A.mult, ["TB", "OB"], ["TH"])
     ts(T.PM[:], T.M0[:, 0:4], P15, None, A.is_equal, None, ["M0", "PC"], ["PM"])
     ts(T.WC[:, 4:5], PS4, 2.0, None, A.mult, None, ["PC"], ["WC4"])
     ts(T.C8[:], T.M0[:, 0:8], -1.0, 8.0, A.mult, A.add, ["M0"], ["C8"])
     ts(T.WC[:, 0:1], T.PM[:, 0:1], -4096.0, None, A.mult, None, ["PM"], ["WC0"])
-    ts(T.UT[:], T.IB[:], T.PM[:, 2:3], T.PM[:, 3:4], A.mult, A.add, ["IB", "PM"], ["UT"])
-    ts(T.U0[:], T.IA[:], T.PM[:, 1:2], None, A.mult, None, ["IA", "PM"], ["U0"])
-    ts(T.WC[:, 1:2], T.PM[:, 1:2], 16.0, T.WC[:, 0:1], A.mult, A.add, ["PM", "WC0"], ["WC1"])
-    ts(T.C8[:], T.C8[:], T.PM[:, 0:1], None, A.mult, None, ["PM", "C8"], ["C8"])
-    tt(T.U0[:], T.U0[:], T.UT[:], A.add, ["U0", "UT"], ["U0"])
-    ts(T.WC[:, 2:3], T.PM[:, 2:3], 1.0, T.WC[:, 1:2], A.mult, A.add, ["PM", "WC1"], ["WC2"])
     for b in range(4):
         ts(T.WC[:, 5 + b:6 + b], T.PM[:, 1:2], 8.0 * b, None, A.mult, None, ["PM"], ["WB%d" % b])
+    ts(T.WC[:, 1:2], T.PM[:, 1:2], 16.0, T.WC[:, 0:1], A.mult, A.add, ["PM", "WC0"], ["WC1"])
+    ts(T.C8[:], T.C8[:], T.PM[:, 0:1], None, A.mult, None, ["PM", "C8"], ["C8"])
+    ts(T.WC[:, 2:3], T.PM[:, 2:3], 1.0, T.WC[:, 1:2], A.mult, A.add, ["PM", "WC1"], ["WC2"])
     ts(T.WC[:, 3:4], T.PM[:, 3:4], T.WC[:, 4:5], T.WC[:, 2:3], A.mult, A.add, ["PM", "WC2", "WC4"], ["WC3"])
-    for b in range(4):
-        ts(T.UU[:, 128 * b:128 * b + 128], T.U0[:], T.WC[:, 5 + b:6 + b], None, A.add, None, ["U0", "WB%d" % b],
-           ["UU%d" % b])
-    for r in range(N):
-        op("a", lambda r=r: g.scalar.activation(T.VAL[:, 512 * r:512 * r + 512], T.UU[:], ActivationFunctionType.Identity,
-                                                bias=T.C8[:, r:r + 1]),
-           ["C8", "UU0", "UU1", "UU2", "UU3"], ["VAL%d" % r])
-    ts(T.PW[:, 0:128], T.M16[:], 0.0, T.WC[:, 3:4], A.is_equal, A.mult, ["M16", "WC3"], ["PW0"])
-    ts(T.PW[:, 128:144], T.M16[:, 0:16], 0.0, T.WC[:, 3:4], A.is_equal, A.mult, ["M16", "WC3"], ["PW1"])
-    ts(T.JJ[:, 0:128], T.M0[:], 16.0, P15, A.mult, A.add, ["M0", "PC"], ["JJ0"])
-    ts(T.JJ[:, 128:256], T.JJ[:, 0:128], 2048.0, None, A.add, None, ["JJ0"], ["JJ1"])
+
+    for k in range(E):
+        act(T.BB[:, k * 128:(k + 1) * 128], T.HEQ[:], T.MK[:, k:k + 1], None, ["HEQ", "MK"], ["BB%d" % k])
+    for i in range(2):
+        act(T.CM[:, 8 * i:8 * i + 8], T.ON8[:], T.MK[:, k0 + i:k0 + i + 1], None, ["ON8", "MK", "CM"], ["CM%d" % i])
+    base = float(TOK - BIG - 1)
+    act(T.RC[:, 0:1], T.MK[:, k0 + 1:k0 + 2], float(ROOM), base, ["MK"], ["RC0"])
+    act(T.RC[:, 1:2], T.MK[:, 1:2], float(ROOM), base, ["MK"], ["RC1"])
+    for n, k in enumerate((k0, k0 + 1, 0, 1)):
+        act(T.BF[:, n * 128:(n + 1) * 128], T.HEQ[:], T.MK[:, k:k + 1], None, ["HEQ", "MK"], ["BF%d" % n])
+    act(T.JJ[:, 0:128], T.M0[:], 16.0, P15, ["M0", "PC"], ["JJ0"])
+    act(T.JJ[:, 128:256], T.JJ[:, 0:128], 1.0, 2048.0, ["JJ0"], ["JJ1"])
+    for i in range(2):
+        act(T.SW[:, TOK + ROOM * i:TOK + ROOM * i + CAP], T.BB[:, 0:CAP], 0.0, None, ["BB%d" % k for k in range(15)],
+            ["SW%d" % i])
 
     g.vector.wait_ge(T.sem.le, 32)
-    g.vector.wait_ge(T.sem.li, 7 * len(off_eng))
+    g.vector.wait_ge(T.sem.li, 3 * len(rest) + 4 * quarter)
     V(lambda: g.vector.tensor_copy(T.E1B[:], T.EI[:, :, 0:32]), [], ["E1B"])
-    V(lambda: g.vector.tensor_copy(T.E2B[:], T.EI[:, :, 32:64]), [], ["E2B"])
 
     def oh(k):
         return T.OH[:, k * 256:(k + 1) * 256]
@@ -289,6 +314,9 @@ def rank_program(g, core, T, topo):
             mm(pb(b, n * 256, n * 256 + 256), T.BB[:, k * 128:(k + 1) * 128], T.DC[:], False, n == 1,
                ["BB%d" % k, "DC"], ["pb%d" % b])
 
+    def scan(out, mask, data, r, w):
+        V(lambda: g.vector.tensor_tensor_scan(out, mask, data, 0.0, A.mult, A.add), r, w)
+
     def offsets(out, sin, ri, tag, r):
         mm(out, T.TH[:], sin[:, 31:256:32], True, False, ["TH"] + r, [tag])
         mm(out, T.OB[:], ri[:], False, True, ["OB"] + r, [tag])
@@ -298,25 +326,26 @@ def rank_program(g, core, T, topo):
         mm(pb(7, 0, 256), T.ZP[:, 120 - 8 * k:248 - 8 * k], oh(k), k == 0, k == E - 1, ["ZP", "OH%d" % k], ["pb7"])
     for b in range(3):
         tri(b)
+    scan(T.SIN[:], T.RM[:], pb(7, 0, 256), ["pb7", "RM"], ["SIN"])
+    scan(T.RI[:], T.ON8[:], T.SIN[:, 31:256:32], ["SIN", "ON8"], ["RI"])
+    offsets(pb(7, 256, 264), T.SIN, T.RI, "pb7", ["SIN", "RI"])
+    mm(pb(7, 264, 265), T.CM[:], T.RI[:, 7:8], True, True, ["CM", "CM0", "CM1", "RI"], ["pb7"])
+    for b in range(3, 7):
+        tri(b)
+    V(lambda: g.vector.tensor_copy(T.E2B[:], T.EI[:, :, 32:64]), [], ["E2B"])
+    ts(T.PW[:, 0:128], T.M16[:], 0.0, T.WC[:, 3:4], A.is_equal, A.mult, ["M16", "WC3"], ["PW0"])
+    ts(T.PW[:, 128:144], T.M16[:, 0:16], 0.0, T.WC[:, 3:4], A.is_equal, A.mult, ["M16", "WC3"], ["PW1"])
+    tt(pb(7, 0, 256, 32), T.SIN[:, 0:256:32], pb(7, 256, 264), A.add, ["SIN", "pb7"], ["pb7"])
+    scan(T.SF[:], T.RM[:], pb(7, 0, 256), ["pb7", "RM"], ["SF"])
+    ts(T.DC[:], T.SF[:], float(CAP + 16), float(CAP), A.min, A.subtract, ["SF"], ["DC"])
+    ts(T.C1[:], pb(7, 264, 265), float(CAP), T.RC[:, 1:2], A.min, A.add, ["pb7", "RC1"], ["C1"])
+    act(T.S1[:], T.SF[:], 1.0, T.RC[:, 0:1], ["SF", "RC0"], ["S1"])
     for i in range(2):
         ts(T.THR[:, 256 * i:256 * i + 256], T.E2B[:], float(k0 + i), 1.0e5, A.not_equal, A.mult, ["E2B"], ["THR%d" % i])
     for i in range(2):
-        ts(T.THR[:, 256 * i:256 * i + 256], T.THR[:, 256 * i:256 * i + 256], BIG + 1, None, A.add, None, ["THR%d" % i],
-           ["THR%d" % i])
-    V(lambda: g.vector.tensor_tensor_scan(T.SIN[:], T.RM[:], pb(7, 0, 256), 0.0, A.mult, A.add), ["pb7"] + RMT, ["SIN"])
-    V(lambda: g.vector.tensor_tensor_scan(T.RI[:], T.ON8[:], T.SIN[:, 31:256:32], 0.0, A.mult, A.add), ["SIN", "ON8"],
-      ["RI"])
-    offsets(pb(7, 256, 264), T.SIN, T.RI, "pb7", ["SIN", "RI"])
-    mm(pb(7, 264, 265), T.CM[:], T.RI[:, 7:8], True, True, ["CM", "RI"], ["pb7"])
-    for b in range(3, 7):
-        tri(b)
-    for r in range(N):
-        ts(T.SF[:, 32 * r:32 * r + 32], T.SIN[:, 32 * r:32 * r + 32], pb(7, 256 + r, 257 + r), None, A.add, None,
-           ["SIN", "pb7"], ["SF%d" % r])
-    SFT = ["SF%d" % r for r in range(N)]
-    ts(T.DC[:], T.SF[:], float(CAP + 16), float(CAP), A.min, A.subtract, SFT, ["DC"])
-    ts(T.C1[:], pb(7, 264, 265), float(CAP), T.RC[:, 1:2], A.min, A.add, ["pb7", "RC1"], ["C1"])
-    ts(T.S1[:], T.SF[:], T.RC[:, 0:1], None, A.add, None, SFT + ["RC0"], ["S1"])
+        act(T.THR[:, 256 * i:256 * i + 256], T.THR[:, 256 * i:256 * i + 256], 1.0, BIG + 1, ["THR%d" % i], ["THR%d" % i])
+    act(T.UT[:], T.IB[:], T.PM[:, 2:3], T.PM[:, 3:4], ["IB", "PM"], ["UT"])
+    act(T.U0[:], T.IA[:], T.PM[:, 1:2], None, ["IA", "PM"], ["U0"])
     for b in range(8):
         if b == 7:
             tri(7)
@@ -325,62 +354,70 @@ def rank_program(g, core, T, topo):
             V(lambda: g.vector.tensor_copy(T.ACC[:], pb(0, 0, 512)), ["pb0"], ["ACC"])
         else:
             tt(T.ACC[:], T.ACC[:], pb(b, 0, 512), A.max, ["ACC", "pb%d" % b], ["ACC"])
+        if b == 4:
+            tt(T.U0[:], T.U0[:], T.UT[:], A.add, ["U0", "UT"], ["U0"])
+    for b in range(4):
+        act(T.UU[:, 128 * b:128 * b + 128], T.U0[:], 1.0, T.WC[:, 5 + b:6 + b], ["U0", "WB%d" % b], ["UU%d" % b])
+    for r in range(N):
+        act(T.VAL[:, 512 * r:512 * r + 512], T.UU[:], 1.0, T.C8[:, r:r + 1], ["C8", "UU0", "UU1", "UU2", "UU3"],
+            ["VAL%d" % r])
     mm(pb(0, 0, 512), T.TRI[:], T.OH[:, k0 * 256:k0 * 256 + 512], True, False,
        ["TRI", "OH%d" % k0, "OH%d" % (k0 + 1)], ["pb0"])
     for i in range(2):
         mm(pb(0, 256 * i, 256 * i + 256), T.BF[:, i * 128:(i + 1) * 128], T.S1[:], False, i == 1, ["BF%d" % i, "S1"],
            ["pb0"])
 
-    tt(T.MM[:], T.ACC[:, 0:256], T.ACC[:, 256:512], A.max, ["ACC"], ["MM"])
+    tt(pb(6, 0, 256), T.ACC[:, 0:256], T.ACC[:, 256:512], A.max, ["ACC"], ["pb6"])
     for i in range(2):
-        tt(T.JB[:, 256 * i:256 * i + 256], T.MM[:], T.THR[:, 256 * i:256 * i + 256], A.is_ge, ["MM", "THR%d" % i],
+        tt(T.JB[:, 256 * i:256 * i + 256], pb(6, 0, 256), T.THR[:, 256 * i:256 * i + 256], A.is_ge, ["pb6", "THR%d" % i],
            ["JB%d" % i])
         mm(pb(1, 0, 256), T.ZP[:, 120 - 8 * i:248 - 8 * i], T.JB[:, 256 * i:256 * i + 256], i == 0, i == 1,
            ["ZP", "JB%d" % i], ["pb1"])
     mm(pb(3, 0, 512), T.TRI[:], T.JB[:], True, False, ["TRI", "JB0", "JB1"], ["pb3"])
-    V(lambda: g.vector.tensor_tensor_scan(T.SIN2[:], T.RM[:], pb(1, 0, 256), 0.0, A.mult, A.add), ["pb1"] + RMT, ["SIN2"])
-    V(lambda: g.vector.tensor_tensor_scan(T.RI2[:], T.ON8[:], T.SIN2[:, 31:256:32], 0.0, A.mult, A.add), ["SIN2", "ON8"],
-      ["RI2"])
+    scan(T.SIN2[:], T.RM[:], pb(1, 0, 256), ["pb1", "RM"], ["SIN2"])
+    scan(T.RI2[:], T.ON8[:], T.SIN2[:, 31:256:32], ["SIN2", "ON8"], ["RI2"])
     offsets(pb(2, 0, 8), T.SIN2, T.RI2, "pb2", ["SIN2", "RI2"])
-    for r in range(N):
-        ts(T.S2[:, 32 * r:32 * r + 32], T.SIN2[:, 32 * r:32 * r + 32], pb(2, r, r + 1), T.C1[:], A.add, A.add,
-           ["SIN2", "pb2", "C1"], ["S2%d" % r])
-    S2T = ["S2%d" % r for r in range(N)]
+    ts(T.OF2[:], pb(2, 0, 8), T.C1[:], None, A.add, None, ["pb2", "C1"], ["OF2"])
+    tt(pb(1, 0, 256, 32), T.SIN2[:, 0:256:32], T.OF2[:], A.add, ["SIN2", "OF2"], ["pb1"])
+    scan(T.S2[:], T.RM[:], pb(1, 0, 256), ["pb1", "RM"], ["S2"])
     for i in range(2):
         mm(pb(3, 256 * i, 256 * i + 256), T.BF[:, (2 + i) * 128:(3 + i) * 128], T.S2[:], False, i == 1,
-           ["BF%d" % (2 + i)] + S2T, ["pb3"])
-
-    def taken(bank, G, AA, n):
-        for i in range(2):
-            ts(G[:, 256 * i:256 * i + 256], pb(bank, 256 * i, 256 * i + 256), float(TOK + CAP * (i + 1)), None, A.is_lt,
-               None, ["pb%d" % bank], ["G%d%d" % (n, i)])
-        tt(AA[:], G[:], pb(bank, 0, 512), A.mult, ["G%d0" % n, "G%d1" % n, "pb%d" % bank], ["A%d" % n])
-
-    taken(0, T.G1, T.A1, 1)
-    tt(T.B1[:], T.A1[:, 0:256], T.A1[:, 256:512], A.max, ["A1"], ["B1"])
-    tt(T.B1[:], T.B1[:], T.JJ[:], A.max, ["B1", "JJ0", "JJ1"], ["B1"])
-    taken(3, T.G2, T.A2, 2)
-    tt(T.B2[:], T.A2[:, 0:256], T.A2[:, 256:512], A.max, ["A2"], ["B2"])
-    tt(T.B2[:], T.B2[:], T.B1[:], A.max, ["B2", "B1"], ["B2"])
+           ["BF%d" % (2 + i), "S2"], ["pb3"])
+    for i in range(2):
+        ts(T.G1[:, 256 * i:256 * i + 256], pb(0, 256 * i, 256 * i + 256), float(TOK + ROOM * i + CAP), None, A.is_lt,
+           None, ["pb0"], ["G1%d" % i])
+    tt(pb(5, 0, 512), T.G1[:], pb(0, 0, 512), A.mult, ["G10", "G11", "pb0"], ["pb5"])
+    tt(T.B1[:], T.JJ[:], pb(5, 0, 256), A.max, ["pb5", "JJ0", "JJ1"], ["B1"])
+    tt(T.B1[:], T.B1[:], pb(5, 256, 512), A.max, ["B1", "pb5"], ["B1"])
+    tt(T.B2[:], T.B1[:], pb(3, 0, 256), A.max, ["B1", "pb3"], ["B2"])
+    tt(T.B2[:], T.B2[:], pb(3, 256, 512), A.max, ["B2", "pb3"], ["B2"])
     V(lambda: g.vector.tensor_copy(T.OFF[:], T.B2[:]), ["B2"], ["OFF"])
 
-    V(lambda: g.vector.tensor_copy(T.SW[:, 0:TOK + SLOTS].indirect(T.OFF[:, 0:256]), T.VAL[:]),
-      ["OFF"] + ["VAL%d" % r for r in range(N)], ["SW"])
-    for q in range(16):
-        mm(pb(4, 0, SLOTS // 16), T.PW[:, 16 - q:144 - q], T.SW[:, TOK + q:TOK + SLOTS:16], q == 0, q == 15,
-           ["PW0", "PW1", "SW"], ["pb4"])
-    ts(T.LST[:], pb(4, 0, SLOTS // 16), float(N * TOK), None, A.add, None, ["pb4"], ["LST"])
+    V(lambda: g.vector.tensor_copy(T.SW[:, 0:TOK + 2 * ROOM].indirect(T.OFF[:, 0:256]), T.VAL[:]),
+      ["OFF", "SW0", "SW1"] + ["VAL%d" % r for r in range(N)], ["SW"])
+    half = CAP // 16
+    for i in range(2):
+        for q in range(16):
+            mm(pb(4 + i, 0, half), T.PW[:, 16 - q:144 - q], T.SW[:, TOK + ROOM * i + q:TOK + ROOM * i + CAP:16], q == 0,
+               q == 15, ["PW0", "PW1", "SW"], ["pb%d" % (4 + i)])
 
-    n_x = NCH * (len(rest[1::2]) + len(off_eng) + 4 * (len(all_eng) // 4))
-    for q in ("v", "a"):
-        for i in range(NCH):
-            eng[q].wait_ge(T.sem["lx%d" % i], 16)
-            eng[q].wait_ge(T.sem["f%d" % i], len(rest[0::2]))
-        eng[q].wait_ge(T.sem.xin, n_x)
+    direct = NCH - len(VIA)
+    n_x = direct * (len(rest[1::2]) + len(off_eng)) + NCH * 4 * quarter + len(VIA) * 3 * quarter
     nst = 0
     for n in range(SLOTS // GCH):
         a, b = n * GCH, (n + 1) * GCH
-        src, out, tags = T.WIN[:, 0:N * TOK + 8].indirect(T.LST[:, a // 16:b // 16]), T.YB[:, a:b], ["LST", "WZ"]
+        i = a // CAP
+        if n % 2 == 0:
+            ts(T.LST[:, i * half:(i + 1) * half], pb(4 + i, 0, half), float(N * TOK), None, A.add, None,
+               ["pb%d" % (4 + i)], ["LST%d" % i])
+        if n == 0:
+            for q in ("v", "a"):
+                for c in range(NCH):
+                    eng[q].wait_ge(T.sem["lx%d" % c], 16)
+                    if c not in VIA:
+                        eng[q].wait_ge(T.sem["f%d" % c], len(rest[0::2]))
+                eng[q].wait_ge(T.sem.xin, n_x)
+        src, out, tags = T.WIN[:, 0:N * TOK + 8].indirect(T.LST[:, a // 16:b // 16]), T.YB[:, a:b], ["LST%d" % i, "WZ"]
         if n % 2 == 0:
             V(lambda: g.vector.tensor_copy(out, src), tags, ["Y%d" % n])
         else:

import numpy as np
from concourse.bass import DstId, RemoteDMATransfer
from concourse.mybir import dt, AluOpType, AxisListType, ActivationFunctionType

N, TOK, E, CAP, CAPP = 8, 4096, 16, 1920, 512
SLOTS = 2 * CAP
NSIM = 64
CHUNKS = [384, 768, 768, 768, 768, 640]
STARTS = [sum(CHUNKS[:i]) for i in range(len(CHUNKS))]
NCH = len(CHUNKS)
VIA = [0]
CUT = [1, 2, 3, 4, 5]
BIG = 32768.0
ROOM = CAP + N * CAPP
GCH = 960

SCRATCH = {
    "WIN": ("sbuf", [128, N * TOK + 8], "float32"),
    "YB": ("sbuf", [128, SLOTS], "float32"),
    "EI": ("sbuf", [128, N, 64], "int32"),
    "PS": ("psum", [128, 4096], "float32"),
    "PI": ("sbuf", [128, 1], "int32"),
    "PJ": ("sbuf", [128, 4], "int32"),
    "OFF": ("sbuf", [128, 256], "uint16"),
    "SW": ("sbuf", [128, TOK + 2 * ROOM], "bfloat16"),
    "LST": ("sbuf", [128, SLOTS // 16], "uint16"),
}
for _n, _w in (("E1B", 256), ("E2B", 256), ("OH", E * 256), ("BB", E * 128), ("ZP", 248), ("TRI", 128), ("PW", 144),
               ("VAL", 4096), ("DC", 256), ("JB", 512)):
    SCRATCH[_n] = ("sbuf", [128, _w], "bfloat16")
for _n, _w in (("BF", 512), ("PC", 4), ("PF", 1), ("M0", 128), ("M8", 128), ("M8S", 128), ("M16", 128), ("IA", 128),
               ("IB", 128), ("HEQ", 128), ("TA", 128), ("TB", 128), ("OB", 128), ("TH", 128), ("MK", 16), ("CM", 128),
               ("ON8", 8), ("RC", 2), ("PM", 4), ("WC", 12), ("C8", 8), ("U0", 128), ("UT", 128), ("UU", 512),
               ("RM", 256), ("JJ", 256), ("SIN", 256), ("RI", 8), ("SF", 256), ("S1", 256), ("C1", 1), ("THR", 512),
               ("ACC", 512), ("SIN2", 256), ("RI2", 8), ("OF2", 8), ("S2", 256), ("G1", 512), ("B1", 256), ("B2", 256)):
    SCRATCH[_n] = ("sbuf", [128, _w], "float32")
SEMAPHORES = (["le", "li", "lf", "xin", "sent", "sv", "st", "sa", "sg", "yd"]
              + ["lx%d" % i for i in range(NCH)] + ["f%d" % i for i in range(NCH)] + ["h%d" % i for i in range(NCH)]
              + ["o%d" % i for i in range(NCH)] + ["k%d" % i for i in range(NCH)] + ["go%d" % i for i in range(NCH - 1)])


def bits(mask):
    return [b for b in range(mask.bit_length()) if mask >> b & 1]


def unbits(bs):
    return sum(1 << b for b in bs)


def make_routes(cores, topo):
    chips = sorted(set(topo.chip(c) for c in cores))
    on = {ch: [c for c in range(NSIM) if topo.chip(c) == ch] for ch in set(topo.chip(c) for c in range(NSIM))}
    far = {s: [ch for ch in chips if ch != topo.chip(cores[s])][0] for s in range(N)}
    land, relay, peer, cross, via = {}, {}, {}, {}, {}
    for d in (0, 1):
        for ch in chips:
            src = [s for s in range(N) if far[s] == ch and topo.die(cores[s]) == d]
            hel = [c for c in on[ch] if c not in cores and topo.die(c) == d]
            src.sort(key=lambda s: not topo.may_write(cores[s], hel[0]))
            hel.sort(key=lambda c: topo.may_write(c, cores[src[0]]))
            for s, hc in zip(src, hel):
                land[s], relay[s] = hc, None
                if not topo.may_write(cores[s], hc):
                    mid = [m for m in on if topo.mates(m, ch) and topo.same_plane(m, topo.chip(cores[s]))][0]
                    relay[s] = [c for c in on[mid] if topo.die(c) == d and topo.may_write(c, hc)][0]
            own = [s for s in range(N) if topo.chip(cores[s]) == ch and topo.die(cores[s]) == d]
            for s, hc in zip(own, hel):
                via[s] = hc
    for ch in chips:
        die = [[s for s in range(N) if topo.chip(cores[s]) == ch and topo.die(cores[s]) == d] for d in (0, 1)]
        for d in (0, 1):
            for i in (0, 1):
                peer[die[d][i]] = die[d][1 - i]
                cross[die[d][i]] = die[1 - d][i]
    return land, relay, peer, cross, via


def rank_program(g, core, T, topo):
    cores = list(T.cores)
    land, relay, peer, cross, via = make_routes(cores, topo)
    rank = T.rank_of(core)
    sent = [0]

    def ids(cs):
        out = []
        for c in cs:
            rid, pid, _ = topo.addr(c)
            out.append(DstId(rid=rid, pnc=pid))
        return out

    def write(buf, parts):
        trs = []
        for cs, eng, sem in parts:
            trs.append(RemoteDMATransfer(dst_ids=ids(cs), dma_engine_mask=unbits(eng), remote_sem=T.sem[sem],
                                         srcs=[buf], dsts=[buf for _ in cs]))
            sent[0] += len(eng)
        g.remote_dma_fused(trs, local_sem=T.sem.sent)

    def xpart(s, i):
        a = s * TOK + STARTS[i]
        return T.WIN[:, a:a + CHUNKS[i]]

    def pieces(s, i):
        k = 2 if relay[s] is not None and i in CUT else 1
        a, w = s * TOK + STARTS[i], CHUNKS[i] // k
        return [(T.WIN[:, a + j * w:a + (j + 1) * w], ("h%d", "k%d")[j] % i) for j in range(k)]

    off_eng = bits(min(topo.mask(core, c) for c in range(NSIM) if c != core))
    all_eng = bits(max(topo.mask(core, c) for c in range(NSIM) if c != core))
    rest = [b for b in all_eng if b not in off_eng]
    q4 = [all_eng[k::4] for k in range(4)]
    quarter = len(q4[0])

    if rank is None:
        here = [c for c in cores if topo.chip(c) == topo.chip(core)]
        same = [c for c in here if topo.die(c) == topo.die(core)]
        other = [c for c in here if topo.die(c) != topo.die(core)]
        for s in range(N):
            if relay[s] == core:
                g.wait_ge(T.sem.lf, len(off_eng))
                write(T.EI[:, s], [([land[s]], off_eng, "lf")])
            if land[s] == core:
                g.wait_ge(T.sem.lf, len(off_eng))
                write(T.EI[:, s], [([other[0]], q4[0], "li"), ([same[0]], q4[1], "li"),
                                   ([other[1]], q4[2], "li"), ([same[1]], q4[3], "li")])
        for s in range(N):
            if via[s] == core:
                for i in VIA:
                    g.wait_ge(T.sem["o%d" % i], len(rest))
                    write(xpart(s, i), [([other[0]], q4[0], "xin"), ([cores[peer[s]]], q4[1], "xin"),
                                        ([other[1]], q4[2], "xin")])
        for s in range(N):
            if relay[s] == core:
                for i in range(NCH):
                    for p, first in pieces(s, i):
                        g.wait_ge(T.sem[first], len(off_eng))
                        write(p, [([land[s]], off_eng, "h%d" % i)])
            if land[s] == core:
                for i in range(NCH):
                    g.wait_ge(T.sem["h%d" % i], len(pieces(s, i)) * len(off_eng))
                    write(xpart(s, i), [([other[0]], q4[0], "xin"), ([same[0]], q4[1], "xin"),
                                        ([other[1]], q4[2], "xin"), ([same[1]], q4[3], "xin")])
        if sent[0]:
            g.wait_ge(T.sem.sent, sent[0])
        return

    g.sync.dma_start(T.EI[:, rank, 0:32], T.e1[:]).then_inc(T.sem.le, 16)
    g.scalar.dma_start(T.EI[:, rank, 32:64], T.e2[:]).then_inc(T.sem.le, 16)
    for i in range(NCH):
        if i:
            g.sync.wait_ge(T.sem["go%d" % (i - 1)], 1)
        g.sync.dma_start(xpart(rank, i), T.x[:, STARTS[i]:STARTS[i] + CHUNKS[i]]).then_inc(T.sem["lx%d" % i], 16)

    eng = {"v": g.vector, "t": g.tensor, "a": g.scalar, "g": g}
    sem = {"v": T.sem.sv, "t": T.sem.st, "a": T.sem.sa, "g": T.sem.sg}
    cnt = {"v": 0, "t": 0, "a": 0, "g": 0}
    seen, wr, rd = {}, {}, {}

    def op(q, fn, r, w):
        need = {}

        def dep(x):
            if not (x[0] == q and q == "t"):
                need[x[0]] = max(need.get(x[0], 0), x[1])
        for t in r:
            if t in wr:
                dep(wr[t])
        for t in w:
            if t in wr:
                dep(wr[t])
            for x in rd.get(t, {}).items():
                dep(x)
        for k in sorted(need):
            if seen.get((q, k), 0) < need[k]:
                eng[q].wait_ge(sem[k], need[k])
                seen[(q, k)] = need[k]
        fn().then_inc(sem[q], 1)
        cnt[q] += 1
        for t in r:
            rd.setdefault(t, {})[q] = cnt[q]
        for t in w:
            wr[t] = (q, cnt[q])
            rd[t] = {}

    def V(fn, r, w):
        op("v", fn, r, w)

    def ts(out, in0, s1, s2, op0, op1, r, w):
        if op1 is None:
            V(lambda: g.vector.tensor_scalar(out, in0, s1, s2, op0), r, w)
        else:
            V(lambda: g.vector.tensor_scalar(out, in0, s1, s2, op0, op1), r, w)

    def tt(out, a, b, o, r, w):
        V(lambda: g.vector.tensor_tensor(out, a, b, o), r, w)

    def act(out, in_, scale, bias, r, w):
        if bias is None:
            op("a", lambda: g.scalar.activation(out, in_, ActivationFunctionType.Copy, scale=scale), r, w)
        else:
            op("a", lambda: g.scalar.activation(out, in_, ActivationFunctionType.Identity, bias=bias, scale=scale), r, w)

    def mm(out, lhsT, rhs, start, stop, r, w):
        op("t", lambda: g.tensor.matmul(out, lhsT, rhs, start, stop), r, w)

    def iota(out, pattern, cm, w):
        op("g", lambda: g.iota(out, pattern, 0, cm, allow_small_or_imprecise_dtypes=True), [], [w])

    def pb(b, x, y, step=1):
        return T.PS[:, 512 * b + x:512 * b + y:step]

    A = AluOpType
    k0 = 2 * rank

    iota(T.PI[:], [[1, 1]], 1, "PI")
    iota(T.M8[:], [[0, 16], [1, 8]], 0, "M8")
    iota(T.M0[:], [[1, 128]], 0, "M0")
    iota(T.M8S[:], [[1, 16], [0, 8]], 0, "M8S")
    near = [c for c in cores if topo.chip(c) == topo.chip(core) and c != core]
    out_to = relay[rank] if relay[rank] is not None else land[rank]
    g.wait_ge(T.sem.le, 32)
    write(T.EI[:, rank], [([out_to], off_eng, "lf")])
    write(T.EI[:, rank], [(near, rest, "li")])
    g.sem_inc(T.sem.go0, 1)
    for i in range(NCH):
        g.wait_ge(T.sem["lx%d" % i], 16)
        if i in VIA:
            local = [([via[rank]], rest, "o%d" % i)]
        else:
            local = [([cores[cross[rank]]], rest[0::2], "f%d" % i), ([cores[peer[rank]]], rest[1::2], "xin")]
        ps = pieces(rank, i)
        if len(ps) == 1:
            write(xpart(rank, i), [([out_to], off_eng, ps[0][1])] + local)
        else:
            for p, first in ps:
                write(p, [([out_to], off_eng, first)])
            write(xpart(rank, i), local)
        if i + 1 < NCH - 1:
            g.sem_inc(T.sem["go%d" % (i + 1)], 1)
        if i == 0:
            iota(T.M16[:], [[0, 8], [1, 16]], 0, "M16")
        if i == 1:
            iota(T.IA[:], [[1, 8], [0, 2], [32, 8]], 0, "IA")
            iota(T.IB[:], [[0, 8], [1, 2], [0, 8]], 0, "IB")
    got = [s for s in range(N) if cross[s] == rank][0]
    for i in range(NCH):
        if i not in VIA:
            g.wait_ge(T.sem["f%d" % i], len(rest[0::2]))
            write(xpart(got, i), [([cores[peer[rank]]], off_eng, "xin")])

    ts(T.PJ[:, 0:1], T.PI[:], 7, None, A.bitwise_and, None, ["PI"], ["PJ0"])
    ts(T.PJ[:, 1:2], T.PI[:], 3, None, A.arith_shift_right, None, ["PI"], ["PJ1"])
    ts(T.PJ[:, 2:3], T.PI[:], 15, None, A.bitwise_and, None, ["PI"], ["PJ2"])
    ts(T.PJ[:, 3:4], T.PI[:], 4, None, A.arith_shift_right, None, ["PI"], ["PJ3"])
    V(lambda: g.vector.tensor_copy(T.PC[:], T.PJ[:]), ["PJ0", "PJ1", "PJ2", "PJ3"], ["PC"])
    P7, PS3, P15, PS4 = (T.PC[:, i:i + 1] for i in range(4))
    V(lambda: g.vector.tensor_copy(T.PF[:], T.PI[:]), ["PI"], ["PF"])
    ts(T.HEQ[:], T.M8[:], P7, None, A.is_equal, None, ["M8", "PC"], ["HEQ"])
    ts(T.MK[:], T.M0[:, 0:16], PS3, None, A.is_equal, None, ["M0", "PC"], ["MK"])
    V(lambda: g.vector.memset(T.ZP[:], 0.0), [], ["ZP"])
    V(lambda: g.vector.memset(T.CM[:], 0.0), [], ["CM"])
    V(lambda: g.vector.memset(T.ON8[:], 1.0), [], ["ON8"])
    V(lambda: g.vector.memset(T.RM[:], 1.0), [], ["RM"])
    V(lambda: g.vector.tensor_copy(T.ZP[:, 120:128], T.HEQ[:, 0:8]), ["HEQ"], ["ZP"])
    ts(T.TA[:], T.M0[:], T.PF[:], None, A.is_lt, None, ["M0", "PF"], ["TA"])
    ts(T.TB[:], T.M0[:], T.PF[:], BIG, A.is_equal, A.mult, ["M0", "PF"], ["TB"])
    ts(T.OB[:], T.M8S[:], PS3, None, A.is_equal, None, ["M8S", "PC"], ["OB"])
    tt(T.TA[:], T.TA[:], T.HEQ[:], A.mult, ["TA", "HEQ"], ["TA"])
    V(lambda: g.vector.memset(T.RM[:, 0:256:32], 0.0), [], ["RM"])
    tt(T.TRI[:], T.TB[:], T.TA[:], A.subtract, ["TA", "TB"], ["TRI"])
    ts(T.TB[:], T.M0[:], T.PF[:], -1.0, A.is_le, A.mult, ["M0", "PF"], ["TB"])
    V(lambda: g.vector.memset(T.WIN[:, N * TOK:], 0.0), [], ["WZ"])
    tt(T.TH[:], T.TB[:], T.OB[:], A.mult, ["TB", "OB"], ["TH"])
    ts(T.PM[:], T.M0[:, 0:4], P15, None, A.is_equal, None, ["M0", "PC"], ["PM"])
    ts(T.WC[:, 4:5], PS4, 2.0, None, A.mult, None, ["PC"], ["WC4"])
    ts(T.C8[:], T.M0[:, 0:8], -1.0, 8.0, A.mult, A.add, ["M0"], ["C8"])
    ts(T.WC[:, 0:1], T.PM[:, 0:1], -4096.0, None, A.mult, None, ["PM"], ["WC0"])
    for b in range(4):
        ts(T.WC[:, 5 + b:6 + b], T.PM[:, 1:2], 8.0 * b, None, A.mult, None, ["PM"], ["WB%d" % b])
    ts(T.WC[:, 1:2], T.PM[:, 1:2], 16.0, T.WC[:, 0:1], A.mult, A.add, ["PM", "WC0"], ["WC1"])
    ts(T.C8[:], T.C8[:], T.PM[:, 0:1], None, A.mult, None, ["PM", "C8"], ["C8"])
    ts(T.WC[:, 2:3], T.PM[:, 2:3], 1.0, T.WC[:, 1:2], A.mult, A.add, ["PM", "WC1"], ["WC2"])
    ts(T.WC[:, 3:4], T.PM[:, 3:4], T.WC[:, 4:5], T.WC[:, 2:3], A.mult, A.add, ["PM", "WC2", "WC4"], ["WC3"])

    for k in range(E):
        act(T.BB[:, k * 128:(k + 1) * 128], T.HEQ[:], T.MK[:, k:k + 1], None, ["HEQ", "MK"], ["BB%d" % k])
    for i in range(2):
        act(T.CM[:, 8 * i:8 * i + 8], T.ON8[:], T.MK[:, k0 + i:k0 + i + 1], None, ["ON8", "MK", "CM"], ["CM%d" % i])
    base = float(TOK - BIG - 1)
    act(T.RC[:, 0:1], T.MK[:, k0 + 1:k0 + 2], float(ROOM), base, ["MK"], ["RC0"])
    act(T.RC[:, 1:2], T.MK[:, 1:2], float(ROOM), base, ["MK"], ["RC1"])
    for n, k in enumerate((k0, k0 + 1, 0, 1)):
        act(T.BF[:, n * 128:(n + 1) * 128], T.HEQ[:], T.MK[:, k:k + 1], None, ["HEQ", "MK"], ["BF%d" % n])
    act(T.JJ[:, 0:128], T.M0[:], 16.0, P15, ["M0", "PC"], ["JJ0"])
    act(T.JJ[:, 128:256], T.JJ[:, 0:128], 1.0, 2048.0, ["JJ0"], ["JJ1"])
    for i in range(2):
        act(T.SW[:, TOK + ROOM * i:TOK + ROOM * i + CAP], T.BB[:, 0:CAP], 0.0, None, ["BB%d" % k for k in range(15)],
            ["SW%d" % i])

    g.vector.wait_ge(T.sem.le, 32)
    g.vector.wait_ge(T.sem.li, 3 * len(rest) + 4 * quarter)
    V(lambda: g.vector.tensor_copy(T.E1B[:], T.EI[:, :, 0:32]), [], ["E1B"])

    def oh(k):
        return T.OH[:, k * 256:(k + 1) * 256]

    def tri(b):
        mm(pb(b, 0, 512), T.TRI[:], T.OH[:, b * 512:(b + 1) * 512], True, False,
           ["TRI", "OH%d" % (2 * b), "OH%d" % (2 * b + 1)], ["pb%d" % b])

    def add_columns(b):
        for n in range(2):
            k = 2 * b + n
            mm(pb(b, n * 256, n * 256 + 256), T.BB[:, k * 128:(k + 1) * 128], T.DC[:], False, n == 1,
               ["BB%d" % k, "DC"], ["pb%d" % b])

    def scan(out, mask, data, r, w):
        V(lambda: g.vector.tensor_tensor_scan(out, mask, data, 0.0, A.mult, A.add), r, w)

    def offsets(out, sin, ri, tag, r):
        mm(out, T.TH[:], sin[:, 31:256:32], True, False, ["TH"] + r, [tag])
        mm(out, T.OB[:], ri[:], False, True, ["OB"] + r, [tag])

    for k in range(E):
        ts(oh(k), T.E1B[:], float(k), None, A.is_equal, None, ["E1B"], ["OH%d" % k])
        mm(pb(7, 0, 256), T.ZP[:, 120 - 8 * k:248 - 8 * k], oh(k), k == 0, k == E - 1, ["ZP", "OH%d" % k], ["pb7"])
    for b in range(3):
        tri(b)
    scan(T.SIN[:], T.RM[:], pb(7, 0, 256), ["pb7", "RM"], ["SIN"])
    scan(T.RI[:], T.ON8[:], T.SIN[:, 31:256:32], ["SIN", "ON8"], ["RI"])
    offsets(pb(7, 256, 264), T.SIN, T.RI, "pb7", ["SIN", "RI"])
    mm(pb(7, 264, 265), T.CM[:], T.RI[:, 7:8], True, True, ["CM", "CM0", "CM1", "RI"], ["pb7"])
    for b in range(3, 7):
        tri(b)
    V(lambda: g.vector.tensor_copy(T.E2B[:], T.EI[:, :, 32:64]), [], ["E2B"])
    ts(T.PW[:, 0:128], T.M16[:], 0.0, T.WC[:, 3:4], A.is_equal, A.mult, ["M16", "WC3"], ["PW0"])
    ts(T.PW[:, 128:144], T.M16[:, 0:16], 0.0, T.WC[:, 3:4], A.is_equal, A.mult, ["M16", "WC3"], ["PW1"])
    tt(pb(7, 0, 256, 32), T.SIN[:, 0:256:32], pb(7, 256, 264), A.add, ["SIN", "pb7"], ["pb7"])
    scan(T.SF[:], T.RM[:], pb(7, 0, 256), ["pb7", "RM"], ["SF"])
    ts(T.DC[:], T.SF[:], float(CAP + 16), float(CAP), A.min, A.subtract, ["SF"], ["DC"])
    ts(T.C1[:], pb(7, 264, 265), float(CAP), T.RC[:, 1:2], A.min, A.add, ["pb7", "RC1"], ["C1"])
    act(T.S1[:], T.SF[:], 1.0, T.RC[:, 0:1], ["SF", "RC0"], ["S1"])
    for i in range(2):
        ts(T.THR[:, 256 * i:256 * i + 256], T.E2B[:], float(k0 + i), 1.0e5, A.not_equal, A.mult, ["E2B"], ["THR%d" % i])
    for i in range(2):
        act(T.THR[:, 256 * i:256 * i + 256], T.THR[:, 256 * i:256 * i + 256], 1.0, BIG + 1, ["THR%d" % i], ["THR%d" % i])
    act(T.UT[:], T.IB[:], T.PM[:, 2:3], T.PM[:, 3:4], ["IB", "PM"], ["UT"])
    act(T.U0[:], T.IA[:], T.PM[:, 1:2], None, ["IA", "PM"], ["U0"])
    for b in range(8):
        if b == 7:
            tri(7)
        add_columns(b)
        if b == 0:
            V(lambda: g.vector.tensor_copy(T.ACC[:], pb(0, 0, 512)), ["pb0"], ["ACC"])
        else:
            tt(T.ACC[:], T.ACC[:], pb(b, 0, 512), A.max, ["ACC", "pb%d" % b], ["ACC"])
        if b == 4:
            tt(T.U0[:], T.U0[:], T.UT[:], A.add, ["U0", "UT"], ["U0"])
    for b in range(4):
        act(T.UU[:, 128 * b:128 * b + 128], T.U0[:], 1.0, T.WC[:, 5 + b:6 + b], ["U0", "WB%d" % b], ["UU%d" % b])
    for r in range(N):
        act(T.VAL[:, 512 * r:512 * r + 512], T.UU[:], 1.0, T.C8[:, r:r + 1], ["C8", "UU0", "UU1", "UU2", "UU3"],
            ["VAL%d" % r])
    mm(pb(0, 0, 512), T.TRI[:], T.OH[:, k0 * 256:k0 * 256 + 512], True, False,
       ["TRI", "OH%d" % k0, "OH%d" % (k0 + 1)], ["pb0"])
    for i in range(2):
        mm(pb(0, 256 * i, 256 * i + 256), T.BF[:, i * 128:(i + 1) * 128], T.S1[:], False, i == 1, ["BF%d" % i, "S1"],
           ["pb0"])

    tt(pb(6, 0, 256), T.ACC[:, 0:256], T.ACC[:, 256:512], A.max, ["ACC"], ["pb6"])
    for i in range(2):
        tt(T.JB[:, 256 * i:256 * i + 256], pb(6, 0, 256), T.THR[:, 256 * i:256 * i + 256], A.is_ge, ["pb6", "THR%d" % i],
           ["JB%d" % i])
        mm(pb(1, 0, 256), T.ZP[:, 120 - 8 * i:248 - 8 * i], T.JB[:, 256 * i:256 * i + 256], i == 0, i == 1,
           ["ZP", "JB%d" % i], ["pb1"])
    mm(pb(3, 0, 512), T.TRI[:], T.JB[:], True, False, ["TRI", "JB0", "JB1"], ["pb3"])
    scan(T.SIN2[:], T.RM[:], pb(1, 0, 256), ["pb1", "RM"], ["SIN2"])
    scan(T.RI2[:], T.ON8[:], T.SIN2[:, 31:256:32], ["SIN2", "ON8"], ["RI2"])
    offsets(pb(2, 0, 8), T.SIN2, T.RI2, "pb2", ["SIN2", "RI2"])
    ts(T.OF2[:], pb(2, 0, 8), T.C1[:], None, A.add, None, ["pb2", "C1"], ["OF2"])
    tt(pb(1, 0, 256, 32), T.SIN2[:, 0:256:32], T.OF2[:], A.add, ["SIN2", "OF2"], ["pb1"])
    scan(T.S2[:], T.RM[:], pb(1, 0, 256), ["pb1", "RM"], ["S2"])
    for i in range(2):
        mm(pb(3, 256 * i, 256 * i + 256), T.BF[:, (2 + i) * 128:(3 + i) * 128], T.S2[:], False, i == 1,
           ["BF%d" % (2 + i), "S2"], ["pb3"])
    for i in range(2):
        ts(T.G1[:, 256 * i:256 * i + 256], pb(0, 256 * i, 256 * i + 256), float(TOK + ROOM * i + CAP), None, A.is_lt,
           None, ["pb0"], ["G1%d" % i])
    tt(pb(5, 0, 512), T.G1[:], pb(0, 0, 512), A.mult, ["G10", "G11", "pb0"], ["pb5"])
    tt(T.B1[:], T.JJ[:], pb(5, 0, 256), A.max, ["pb5", "JJ0", "JJ1"], ["B1"])
    tt(T.B1[:], T.B1[:], pb(5, 256, 512), A.max, ["B1", "pb5"], ["B1"])
    tt(T.B2[:], T.B1[:], pb(3, 0, 256), A.max, ["B1", "pb3"], ["B2"])
    tt(T.B2[:], T.B2[:], pb(3, 256, 512), A.max, ["B2", "pb3"], ["B2"])
    V(lambda: g.vector.tensor_copy(T.OFF[:], T.B2[:]), ["B2"], ["OFF"])

    V(lambda: g.vector.tensor_copy(T.SW[:, 0:TOK + 2 * ROOM].indirect(T.OFF[:, 0:256]), T.VAL[:]),
      ["OFF", "SW0", "SW1"] + ["VAL%d" % r for r in range(N)], ["SW"])
    half = CAP // 16
    for i in range(2):
        for q in range(16):
            mm(pb(4 + i, 0, half), T.PW[:, 16 - q:144 - q], T.SW[:, TOK + ROOM * i + q:TOK + ROOM * i + CAP:16], q == 0,
               q == 15, ["PW0", "PW1", "SW"], ["pb%d" % (4 + i)])

    direct = NCH - len(VIA)
    n_x = direct * (len(rest[1::2]) + len(off_eng)) + NCH * 4 * quarter + len(VIA) * 3 * quarter
    nst = 0
    for n in range(SLOTS // GCH):
        a, b = n * GCH, (n + 1) * GCH
        i = a // CAP
        if n % 2 == 0:
            ts(T.LST[:, i * half:(i + 1) * half], pb(4 + i, 0, half), float(N * TOK), None, A.add, None,
               ["pb%d" % (4 + i)], ["LST%d" % i])
        if n == 0:
            for q in ("v", "a"):
                for c in range(NCH):
                    eng[q].wait_ge(T.sem["lx%d" % c], 16)
                    if c not in VIA:
                        eng[q].wait_ge(T.sem["f%d" % c], len(rest[0::2]))
                eng[q].wait_ge(T.sem.xin, n_x)
        src, out, tags = T.WIN[:, 0:N * TOK + 8].indirect(T.LST[:, a // 16:b // 16]), T.YB[:, a:b], ["LST%d" % i, "WZ"]
        if n % 2 == 0:
            V(lambda: g.vector.tensor_copy(out, src), tags, ["Y%d" % n])
        else:
            op("a", lambda: g.scalar.activation(out, src, ActivationFunctionType.Copy), tags, ["Y%d" % n])
        q, c = wr["Y%d" % n]
        g.sync.wait_ge(sem[q], c)
        g.sync.dma_start(T.y[:, a:b], out).then_inc(T.sem.yd, 16)
        nst += 16
    g.sync.wait_ge(T.sem.yd, nst)
    for q in ("v", "t", "a", "g"):
        g.wait_ge(sem[q], cnt[q])
    g.wait_ge(T.sem.sent, sent[0])
